import numpy as np, ml_dtypes
CORES = [66,74,82,90,194,202,210,218]
N = 8
import mx_ref
BF = ml_dtypes.bfloat16
def gentries(a):
    return np.ascontiguousarray(a.reshape(8, 16, -1).transpose(0, 2, 1)).reshape(8, -1)
def gtable(e):
    e = np.asarray(e); return np.ascontiguousarray(e.reshape(8, -1, 16).transpose(0, 2, 1)).reshape(128, -1).astype(np.int32)
def gcols(t, e):
    v = np.concatenate([t.reshape(8, 16, -1, 4), np.zeros((8, 16, 1, 4), BF)], axis=2)
    return np.ascontiguousarray(np.stack([v[g][:, e[g]] for g in range(8)])).reshape(128, -1)
def tile(rs):
    return np.stack(rs, axis=2).reshape(128, -1).astype(BF)
def pick(q, e):
    c = np.concatenate([q[0].reshape(128, -1, 4), np.zeros((128, 1, 4), np.uint8)], axis=1); s = np.concatenate([q[1], np.ones((16, 1), np.uint8)], axis=1)
    return (np.ascontiguousarray(c[:, e].reshape(128, -1)), np.ascontiguousarray(s[:, e]))
def join(*qs):
    return (np.concatenate([q[0] for q in qs], axis=1), np.concatenate([q[1] for q in qs], axis=1))
def put(q, e, v):
    c, s = q[0].reshape(128, -1, 4).copy(), q[1].copy(); c[:, e] = v[0].reshape(128, -1, 4); s[:, e] = v[1]
    return (c.reshape(128, -1), s)
def pk(c, s):
    return (np.ascontiguousarray(c), mx_ref.live(s))
def emit(q):
    return q[0], q[1]
def packed(v, rng):
    q = [mx_ref.quantize(np.ascontiguousarray(v[r])) for r in range(N)]
    return np.stack([a for a, b in q]), np.stack([mx_ref.plane(b, rng) for a, b in q])
def values_of_codes():
    e, c = np.zeros((128, 128, 4), np.float32), np.zeros((128, 2, 4), np.uint8)
    e[np.arange(128), np.arange(128), 0] = 1
    c[:127, :, 0] = np.arange(256).reshape(2, 128).T[:127]
    return mx_ref.matmul(mx_ref.quantize(e.reshape(128, 512).astype(BF)), (c.reshape(128, 8), np.full((16, 2), 127, np.uint8))).T.reshape(-1).astype(np.float64)
CODE_VALUE, SCALE_VALUE = values_of_codes(), 2.0 ** (np.arange(256) - 127.0)
def decode(q):
    return (CODE_VALUE[q[0]].reshape(16, 8, -1, 4) * SCALE_VALUE[q[1]][:, None, :, None] + 0.0).reshape(128, -1).astype(np.float32)
def f(rng, *shape):
    return mx_ref.flush((rng.standard_normal(shape, dtype=np.float32) * np.exp2(rng.integers(-2, 3, shape[:-1] + (1,)))).astype(BF))
def wide(rng, *shape, cols=0):
    v = rng.standard_normal(shape, dtype=np.float32) * np.exp2(rng.integers(-12, 13, shape)).astype(np.float32)
    if cols: v *= np.repeat(np.exp2(rng.integers(-cols, cols + 1, shape[:-2] + (1, shape[-1] // 4))) * (rng.random(shape[:-2] + (1, shape[-1] // 4)) > 0.0625), 4, axis=-1).astype(np.float32)
    return mx_ref.flush(v.astype(BF))
C, DOUBLINGS = 288, 9
STEP = [4, 1, 2]
def numbers_of(rng):
    return {"x": np.array(f(rng, N, 128, 4 * C)), "u": np.array(f(rng, N, 128, 512)), "v": np.array(f(rng, N, 128, 512))}
def links(rng, far=False):
    l = rng.permuted(np.tile(np.arange(C), (N, 8, 2, 1)), axis=3)
    if far:
        for r in range(N):
            for i, g in enumerate(rng.permutation(8)[:6]):
                o = rng.permutation(C)
                l[r, g, 0, o] = np.append(o[1:], o[[0, C - 1, C // 2][i % 3]])
                if i < 3: l[r, g, 1] = l[r, g, 0]
    return l
def stored(l):
    return {"la": np.stack([gtable(l[r, :, 0]) for r in range(N)]), "lb": np.stack([gtable(l[r, :, 1]) for r in range(N)])}
def layers(rng, still=[]):
    w = np.array(f(rng, N, 128, 2048)).reshape(N, 8, 16, 4, 8, 16, 4)
    for i in still:
        w[:, :, i] = 0
        w[:, :, :, :, :, i] = 0
    return w
def weights(rng, w):
    c, p = packed(np.ascontiguousarray(w).reshape(N, 128, 2048), rng)
    return {"wc": c, "ws": p}
def setup_inputs(rng):
    return {**numbers_of(rng), **stored(links(rng)), **weights(rng, layers(rng))}
def setup_inputs_ties(rng):
    d = numbers_of(rng)
    o = rng.permutation(N)
    k = rng.integers(-2, 3, (N, 8, C))
    k[o[1]] = -rng.integers(1, 5, (8, C))
    far = rng.permutation(8)
    k[o[2], far[:4]] = 1
    k[o[3], rng.permutation(8)[:4]] = -1
    l = links(rng, True)
    way = rng.permutation(C)
    way[-2:] = np.sort(way[-2:])
    for g, end, top in ((far[4], way[-1], way[-1]), (far[5], way[0], 0)):
        l[o[2], g, 0, way] = np.append(way[1:], end)
        l[o[2], g, 1] = np.arange(C)
        k[o[2], g] = 1
        k[o[2], g, top] = 2
    x = d["x"].reshape(N, 8, 16, C, 4)
    x[:, :, 0] = 0
    x[:, :, 0, :, 0] = k.astype(np.float32).astype(BF)
    u = d["u"].reshape(N, 128, 128, 4)
    u[:, :, ::16] = 0
    for r in range(N):
        for h in range(0, 128, 16): u[r, h, h, 0] = 0.0 if r == o[0] else 1.0
    return {"x": x.reshape(N, 128, 4 * C), "u": u.reshape(N, 128, 512), "v": d["v"], **stored(l), **weights(rng, layers(rng, [0]))}
def setup_inputs_near(rng):
    d = numbers_of(rng)
    x = d["x"].astype(np.float32).reshape(N, 8, 16, C, 4)
    x[:, :, 0] = 0
    x[:, :, 8:] = 0
    u = d["u"].reshape(N, 128, 128, 4)
    u[:, :, ::16] = 0
    w = layers(rng, [0, 8, 9, 10, 11, 12, 13, 14, 15])
    o = rng.permutation(N) % 4
    for r in range(N):
        s = rng.integers(0, 16, (8, C))
        digits = ((s[:, :, None] >> np.arange(4)) & 1) * np.exp2(np.arange(4) - 23.0)
        if o[r] < 3: x[r, :, 12, :, 0] = rng.choice([-1.0, 1.0], (8, C)) * 2.0 ** -20
        if o[r] < 2:
            x[r, :, 0, :, 0] = np.where(rng.permutation(8) < 4, -1.0, 1.0)[:, None]
            x[r, :, 8] = digits
            x[r, :, 11, :, 0] = 2.0 ** -10
        elif o[r] == 2: x[r, :, 8] = digits * rng.choice([-1.0, 1.0], (8, C, 1))
        else:
            e = rng.integers(-1, 2, (8, C)) * 2.0 ** -30
            x[r, :, 8, :, 0] = 1.25 * e
            x[r, :, 9, :, 0] = -1.125 * e
            x[r, :, 15, :, 0] = 2.0 ** -30
            for g in range(8):
                w[r, g, 12, 0, g, 10, 0] = 2.0 ** -18
                w[r, g, 14, 0, g, 10, 0] = 2.0 ** -8
        at = [0, C - 1, int(rng.integers(C)), int(rng.integers(C))]
        for g, j in zip(rng.permutation(8)[:4], at): x[r, g, 0, j, 0] = 2.0 ** 29 * rng.choice([-1.0, 1.0])
        k = 1.0 if o[r] == 0 else 2.0 ** -30
        for h in range(0, 128, 16):
            u[r, h, h, 0] = k if o[r] < 2 else 1.0
            if o[r] < 2: u[r, h + 11, h, 0] = k
            if o[r] < 3: u[r, h + 8, h] = k
            else:
                u[r, h + 8, h, 0] = k
                u[r, h + 9, h, 0] = 1.125 * k
                u[r, h + 10, h, 0] = k
    return {"x": x.reshape(N, 128, 4 * C).astype(BF), "u": u.reshape(N, 128, 512), "v": d["v"], **stored(links(rng, True)), **weights(rng, w)}
def setup_inputs_odd(rng):
    d = numbers_of(rng)
    x = (1.0 + (2 * rng.integers(0, 64, (N, 16, 8, C, 4)) + 1) * 2.0 ** -7) * np.exp2(-rng.integers(0, 7, (N, 16, 8, C, 4)).astype(np.float64)) * rng.choice([-1.0, 1.0], (N, 16, 8, C, 4))
    x[:, :, 0, :, 0] = np.where(rng.random((N, 16, C)) < 0.25, 1.875, 1.96875) * 2.0 ** 8
    x[:, ::2, 1, :, 0] = rng.choice([-1.0, 1.0], (N, 8, C)) * (8 + rng.integers(0, 2, (N, 8, C))) * 2.0 ** -8
    u = d["u"].reshape(N, 16, 8, 128, 4)
    u[:, :, :, ::16] = 0
    for g in range(8): u[:, 2 * g, 1, 16 * g, 0] = 1.0
    return {"x": x.astype(np.float32).reshape(N, 128, 4 * C).astype(BF), "u": u.reshape(N, 128, 512), "v": d["v"], **stored(links(rng)), **weights(rng, layers(rng, [0, 8]))}
def setup_inputs_ends(rng):
    d = numbers_of(rng)
    o, e = rng.permutation(N) % 4, rng.permutation(N) % 4
    m = int(rng.integers(8))
    l = links(rng, True)
    small = -(1.0 + 0.125 * rng.integers(0, 8, (N, 8, 16, C, 4)))
    x = -(0.88 + 0.08 * rng.random((N, 8, 16, C, 4))) * 2.0 ** 30
    x[o == 1] *= rng.choice([-1.0, 1.0], (N, 1, 1, C, 1))[o == 1]
    x[o == 2] = small[o == 2] * 2.0 ** -30
    x[o == 3] = d["x"].astype(np.float32).reshape(N, 8, 16, C, 4)[o == 3][:, :, :, :1]
    x[:, m] = small[:, m] * 2.0 ** -20
    u = d["u"].astype(np.float32).reshape(N, 8, 16, 128, 4)
    v = rng.choice([-1.0, 1.0], (N, 128, 512)) * np.where(o < 2, 2.0 ** 30, 2.0 ** -30)[:, None, None]
    w = np.zeros((N, 128, 4, 128, 4), np.float32)
    i = np.arange(128)
    for r in range(N):
        h = rng.permutation(8)
        c = np.where(h < 2, 0.0, h % 2 * 2.0 - 1.0)[:, None]
        if o[r] < 2: u[r, :, :, ::16] = c * (0.9 + 0.1 * rng.random((8, 16, 8, 4))) * 2.0 ** 30
        if o[r] == 2: u[r, :, :, ::16] = c * (1.0 + 0.125 * rng.integers(0, 8, (8, 16, 8, 4))) * 2.0 ** -30
        if o[r] == 3: u[r, :, :, ::16] *= np.abs(c).astype(np.float32)
        k = np.zeros(8)
        if o[r] < 2: k = rng.choice([-1.0, 1.0], 8) * np.array([0.75, 0.5, 2.0 ** -8])[rng.permutation(8) % 3]
        k[m] = 2.0 ** 8
        for b in range(4): w[r, i, b, i, b] = k[i // 16]
        if e[r] < 2:
            l[r, :, e[r]] = C - 1
            l[r, :, 1 - e[r]] = 0
        if e[r] == 2: l[r] = rng.integers(0, C, (8, 2, C))
    u[:, m, :, ::16] = 0
    return {"x": x.astype(np.float32).reshape(N, 128, 4 * C).astype(BF), "u": u.reshape(N, 128, 512).astype(BF), "v": v.astype(np.float32).astype(BF), **stored(l), **weights(rng, w.astype(BF))}
def setup_inputs_spread(rng):
    d = setup_inputs(rng)
    d["x"] = wide(rng, N, 128, 4 * C, cols=6)
    return d
def check_inputs(d):
    b = []
    for k in ("x", "u", "v"):
        a = np.abs(d[k].astype(np.float32))
        if not (np.isfinite(a).all() and ((a == 0) | (a >= 2.0 ** -30) & (a <= 2.0 ** 30)).all()): b.append("a value of " + k)
    for k in ("la", "lb"):
        if not ((d[k] >= 0) & (d[k] < C)).all(): b.append("an entry of " + k)
    none, least, most = [emit(mx_ref.quantize(np.full((128, 16), k, np.float32).astype(BF)))[1][0, 0] for k in (0.0, 2.0 ** -8, 2.0 ** 8)]
    for r in range(N):
        if ((d["wc"][r] == 0x7F) | (d["wc"][r] == 0xFF)).any(): b.append("wc: a code that is no number")
        s = mx_ref.live(d["ws"][r])
        if ((s != none) & ((s < least) | (s > most))).any(): b.append("ws: a scale out of range")
        if (((d["wc"][r].reshape(16, 8, 512, 4) & 0x7F) != 0) & (s == none)[:, None, :, None]).any(): b.append("wc: a code other than zero under the scale of zeros")
    return b
def look(t, e):
    return np.take_along_axis(t, e, axis=1)
def leaders(p):
    low, at = np.tile(np.arange(C), (8, 1)), p
    for k in range(DOUBLINGS):
        low = np.minimum(low, look(low, at))
        at = look(at, at)
    return look(low, at)
def reference(x, u, v, la, lb, wc, ws):
    qu = [mx_ref.quantize(u[r]) for r in range(N)]
    lay = [pk(wc[r], ws[r]) for r in range(N)]
    l0, l1 = [gentries(la[r]) for r in range(N)], [gentries(lb[r]) for r in range(N)]
    now = [x[r] for r in range(N)]
    for step in STEP:
        own, torn, sent = [], [], []
        for r in range(N):
            q = mx_ref.quantize(now[r])
            s = mx_ref.matmul(qu[r], q)[::16] + np.float32(0.0)
            p = np.where(s < 0, l1[r], l0[r])
            lead = leaders(p)
            e = np.where(lead == np.arange(C), lead, p)
            own.append(decode(q).astype(BF))
            torn.append(e)
            z = own[r]
            for k in range(3):
                z = ((z.astype(np.float32) + gcols(z, e).astype(np.float32)) * np.float32(0.5)).astype(BF)
                e = look(e, e)
            sent.append(mx_ref.quantize(z))
            change = look(s, lead) > s
            l0[r], l1[r] = np.where(change, l1[r], l0[r]), np.where(change, l0[r], l1[r])
        for r in range(N):
            z = sent[(r - step) % N]
            h = tile([mx_ref.matmul(pick(lay[r], np.arange(128 * b, 128 * b + 128)), z) * np.float32(0.03125) for b in range(4)])
            now[r] = (own[r].astype(np.float32) + gcols(h, torn[r]).astype(np.float32)).astype(BF)
    y, ls = np.zeros((N, 128, C), np.float32), np.zeros((N, 8, 2 * C), np.float32)
    oc, osc = np.zeros((N, 128, 4 * C), np.uint8), np.zeros((N, 16, C), np.uint8)
    for r in range(N):
        q = mx_ref.quantize(now[r])
        y[r] = mx_ref.matmul(mx_ref.quantize(v[r]), q)
        ls[r] = np.concatenate([l0[r], l1[r]], axis=1)
        oc[r], osc[r] = emit(q)
    return {"y": y, "ls": ls, "oc": oc, "osc": osc}

@@ -1,0 +1,474 @@
+from concourse.mybir import dt, AluOpType, ActivationFunctionType
+
+C = 288
+K = C // 16
+STEP = [4, 1, 2]
+ROUNDS = len(STEP)
+HALF = C // 2
+CUT = 160
+
+SCRATCH = {}
+
+
+def _declare():
+    s = SCRATCH
+    for k in range(ROUNDS + 1):
+        s["xt%d" % k] = ("sbuf", [128, 4 * C], "bfloat16")
+        s["xq%d" % k] = ("sbuf", [128, C], "float8_e4m3fn_x4")
+        s["xs%d" % k] = ("sbuf", [128, C], "uint8")
+    for k in range(ROUNDS):
+        s["aq%d" % k] = ("sbuf", [128, C], "float8_e4m3fn_x4")
+        s["as%d" % k] = ("sbuf", [128, C], "uint8")
+        for n in ("ta", "tb", "td"):
+            s[n + str(k)] = ("sbuf", [128, 32], "uint16")
+        s["zq%d" % k] = ("sbuf", [128, C], "float8_e4m3fn_x4")
+        s["zs%d" % k] = ("sbuf", [128, C], "uint8")
+    for n, w in (("ut", 512), ("vt", 512), ("em", 520), ("en", 520), ("e1", 520), ("e8", 520), ("ic", C), ("m1", C), ("mk", C),
+                 ("dw", C), ("bb", C), ("sa", C), ("sb", C), ("sc", C), ("sd", C), ("se", C), ("fl", C), ("cm", C), ("rb", C), ("rc", C), ("rd", C),
+                 ("q0", C), ("q1", C), ("q2", C), ("xg", C), ("alt", 2 * C), ("st", 12 * C), ("tab", 24 * C), ("ic2", C), ("zd", 6 * C),
+                 ("fo", 4 * C), ("z0", 4 * C), ("z1", 4 * C), ("z2", 4 * C), ("z3", 4 * C), ("gb", 2 * C), ("hb", 4 * C)):
+        s[n] = ("sbuf", [128, w], "bfloat16")
+    for n, w in (("ol", 32 * 9), ("snt", 32 * 3 * ROUNDS), ("uo", 32)):
+        s[n] = ("sbuf", [128, w], "uint16")
+    s["lo"] = ("sbuf", [128, 64], "uint16")
+    for n, w in (("ri", C), ("rr", C), ("pi", 8), ("pj", 8), ("k16", 24), ("uj", 8), ("la32", 24), ("lb32", 24)):
+        s[n] = ("sbuf", [128, w], "int32")
+    for n, w in (("wa", C), ("ssb", C), ("ssc", C), ("fi", C), ("lrep", 2 * C), ("yo", C), ("sc0", 8), ("sc1", 8), ("pf", 8), ("cw", 24), ("tm", 24), ("pw", 24),
+                 ("cp", 24), ("cs", 24), ("pq", 24), ("tn", 24), ("tw", 24), ("xm", 24), ("xd", 24), ("xe", 24), ("l1f", 24), ("lst", 32 * 8)):
+        s[n] = ("sbuf", [128, w], "float32")
+    for n, w in (("uq", 128), ("uq2", 128), ("vq", 128), ("wq", 512), ("c1", 512), ("c8", 512)):
+        s[n] = ("sbuf", [128, w], "float8_e4m3fn_x4")
+        s[n + "s"] = ("sbuf", [128, w], "uint8")
+    for i in range(8):
+        s["ps%d" % i] = ("psum", [128, 512], "float32")
+
+
+_declare()
+SEMAPHORES = (["eV", "eA", "eP", "eG", "lsem"] + ["dx", "du", "dla", "dlb", "dwc", "dws", "dv", "dls", "doc", "dy0", "dy1"] + ["dsc%d" % i for i in range(4)]
+              + ["%s%d" % (n, k) for n in ("rx", "ra", "rb", "rd") for k in range(ROUNDS)])
+
+
+def rank_program(g, core, T, topo):
+    rank = T.rank_of(core)
+    if rank is None:
+        return
+    Q = {"V": g.vector, "A": g.scalar, "P": g.tensor, "G": g, "Y": g.sync}
+    count, known, snap, lastw, readers, total = {}, {q: {} for q in Q}, {}, {}, {}, {}
+
+    def wait_for(q, toks):
+        best = {}
+        for s, n in toks:
+            best[s] = max(n, best.get(s, 0))
+        todo = [(s, n) for s, n in best.items() if known[q].get(s, 0) < n]
+        todo = [t for t in todo if not any(u != t and snap.get(u, {}).get(t[0], 0) >= t[1] for u in todo)]
+        for s, n in todo:
+            Q[q].wait_ge(T.sem[s], n)
+            for a, b in list(snap.get((s, n), {}).items()) + [(s, n)]:
+                known[q][a] = max(b, known[q].get(a, 0))
+
+    def before(q, reads, writes):
+        toks = []
+        for b in reads:
+            if b in lastw:
+                toks.append(lastw[b])
+            if b[:2] == "ps":
+                toks += [t for t in readers.get(b, []) if t[0] != "e" + q]
+        for b in writes:
+            if b in lastw:
+                toks.append(lastw[b])
+            toks += readers.get(b, [])
+        wait_for(q, toks)
+
+    def after(q, tok, reads, writes):
+        snap[tok] = dict(known[q])
+        for b in reads:
+            readers.setdefault(b, []).append(tok)
+        for b in writes:
+            lastw[b] = tok
+            readers[b] = []
+
+    def op(q, reads, writes, call):
+        before(q, reads, writes)
+        s = "e" + q
+        count[s] = count.get(s, 0) + 1
+        call().then_inc(T.sem[s], 1)
+        total[s] = count[s]
+        after(q, (s, count[s]), reads, writes)
+
+    def dma(q, sem, reads, writes, out, in_):
+        before(q, reads, writes)
+        Q[q].dma_start(out, in_).then_inc(T.sem[sem], 16)
+        total[sem] = 16
+        after(q, (sem, 16), reads, writes)
+
+    def send(dst, sem, reads, out, in_):
+        before("G", reads, [])
+        rid, pid = topo.addr(dst, core)
+        g.remote_dma(out, in_, T.sem[sem], T.sem.lsem, pid, rid, topo.mask(core, dst))
+        total["lsem"] = total.get("lsem", 0) + len(topo.engines(core, dst))
+
+    def lands(src, sem, buf, writes=1):
+        n = writes * len(topo.engines(src, core))
+        total[sem] = n
+        for b in buf:
+            lastw[b] = (sem, n)
+            readers[b] = []
+
+    V, A, P = g.vector, g.scalar, g.tensor
+    mult, add, sub, lt, gt, eq, amin = (AluOpType.mult, AluOpType.add, AluOpType.subtract, AluOpType.is_lt, AluOpType.is_gt, AluOpType.is_equal, AluOpType.min)
+    copy = ActivationFunctionType.Copy
+    tables = {n: i * C for i, n in enumerate(["t%d" % i for i in range(9)] + ["l%d" % i for i in range(9)] + ["k%d" % i for i in range(1, 7)])}
+    lists = {n: i * 32 for i, n in enumerate(["lz%d" % i for i in range(ROUNDS + 1)] + ["dz%d" % i for i in range(ROUNDS + 1)])}
+
+    halves = ((0, CUT), (CUT, C))
+    wide = (CUT, C - CUT)
+
+    def parts(n):
+        return [n + "a", n + "b"]
+
+    def full(n, h=None):
+        a, e = (0, C) if h is None else halves[h]
+        if n in tables:
+            return T.tab[:, tables[n] + a:tables[n] + e]
+        return T[n][:, a:e]
+
+    picks = {n: i * 32 for i, n in enumerate(["o%d" % i for i in range(7)] + ["orr", "te"])}
+    sent = {n + str(i): (3 * i + j) * 32 for i in range(ROUNDS) for j, n in enumerate(["pt", "pu", "pv"])}
+
+    def off(n, h=None):
+        if n in picks:
+            a, e = (0, K) if h is None else (halves[h][0] // 16, halves[h][1] // 16)
+            return T.ol[:, picks[n] + a:picks[n] + e]
+        if h is not None:
+            return T[n][:, halves[h][0] // 16:halves[h][1] // 16]
+        if n in sent:
+            return T.snt[:, sent[n]:sent[n] + K]
+        if n in lists:
+            return T.lst[:, lists[n]:lists[n] + K]
+        return T[n][:, 0:K]
+
+    def pl(n, b):
+        return T[n][:, b * C:(b + 1) * C]
+
+    def el(n, b):
+        return T[n][:, b:4 * C:4]
+
+    def ends(n, h=None):
+        a, e = (0, C) if h is None else halves[h]
+        return T[n][:, a + 15:e:16]
+
+    def bank(i, w=C):
+        return T["ps%d" % i][:, 0:w]
+
+    def vtt(out, ok, a, ak, b, bk, o):
+        op("V", ak + bk, ok, lambda: V.tensor_tensor(out, a, b, o))
+
+    def vts(out, a, s1, s2, o1, *o2, w=off, extra=()):
+        op("V", [a] + list(extra), [out], lambda: V.tensor_scalar(w(out), w(a), s1, s2, o1, *o2))
+
+    def scan(d0, d1, out):
+        op("V", [d0, d1], [out], lambda: V.tensor_tensor_scan(full(out), full(d0), full(d1), 0.0, mult, add))
+
+    def offsets(sc, out):
+        op("V", [sc, "sc1"], [out], lambda: V.tensor_scalar(off(out), ends(sc), T.sc1[:, 0:1], 144.25, mult, add))
+
+    def acopy(out, ok, in_, ik, scale=1.0):
+        op("A", ik, ok, lambda: A.activation(out, in_, copy, scale=scale))
+
+    def agather(win, o, out):
+        acopy(full(out), [out], full(win).indirect(off(o)), [win, o])
+
+    def vgather(win, o, out):
+        op("V", [win, o], [out], lambda: V.tensor_copy(full(out), full(win).indirect(off(o))))
+
+    def low(win, o, other, out):
+        vtt(full(out), [out], full(win).indirect(off(o)), [win, o], full(other), [other], amin)
+
+    def again(src, out):
+        op("V", [src], [out], lambda: V.tensor_copy(full(out), full(src)))
+
+    def tiny(out, a, b, o):
+        vtt(off(out), [out], off(a), [a], off(b), [b], o)
+
+    def quant(t, tk, q, s, w=C):
+        op("V", tk, [q], lambda: V.quantize_mx(T[q][:, 0:w], T[s][:, 0:w], T[t][:, 0:4 * w]))
+
+    def scan_part(d0, src, sk, out, h):
+        op("V", [d0] + sk, [parts(out)[h]], lambda: V.tensor_tensor_scan(full(out, h), full(d0, h), full(src, h), 0.0, mult, add))
+
+    def quant_half(t, tk, q, s, h):
+        a, e = halves[h]
+        op("V", tk, [parts(q)[h]], lambda: V.quantize_mx(T[q][:, a:e], T[s][:, a:e], T[t][:, 4 * a:4 * e]))
+
+    def units(e, c, which=range(4)):
+        for b in which:
+            op("V", [e], [c + str(b)], lambda: V.quantize_mx(T[c][:, 128 * b:128 * b + 128], T[c + "s"][:, 128 * b:128 * b + 128],
+                                                             T[e][:, 4 - b:4 - b + 512]))
+
+    def mm(i, l, a, lk, r, rs, rk, c0=0, c1=C):
+        op("P", lk + rk, ["ps%d" % i], lambda: P.matmul_mx(bank(i, c1 - c0), T[l][:, a:a + 128], T[l + "s"][:, a:a + 128],
+                                                           T[r][:, c0:c1], T[rs][:, c0:c1], True, True))
+
+    def iota(out, ok, pattern, base, cm):
+        op("G", [], [ok], lambda: g.iota(out, pattern, base, cm, allow_small_or_imprecise_dtypes=True))
+
+    dma("Y", "dx", [], ["xt0"], T.xt0[:], T.x[:])
+    dma("A", "du", [], ["ut"], T.ut[:], T.u[:])
+    dma("Y", "dla", [], ["la32"], off("la32"), T.la[:])
+    dma("A", "dlb", [], ["lb32"], off("lb32"), T.lb[:])
+    op("V", [], ["em"], lambda: V.memset(T.em[:], 0.125))
+    op("V", [], ["en"], lambda: V.memset(T.en[:], 1.0))
+    iota(T.ri[:], "ri", [[-1, C]], C, 1)
+    iota(T.pi[:, 0:1], "pi", [[0, 1]], 0, 1)
+    iota(T.uj[:, 0:8], "uj", [[16, 8]], 0, 0)
+    iota(off("k16"), "k16", [[16, K]], 0, 0)
+    op("G", ["em"], ["e8"], lambda: g.affine_select(T.e8[:], T.em[:], [[1, 520]], eq, 0.0, -4, -4))
+    iota(T.ic[:], "ic", [[1, C]], -HALF, 0)
+    iota(T.ic2[:], "ic2", [[1, C]], -HALF, 0)
+
+    vts("rr", "ri", 15, None, AluOpType.bitwise_and, w=full)
+    vts("m1", "rr", 1.0, None, amin, w=full)
+    vts("wa", "rr", 15.0, 65535.0, eq, mult, w=full)
+    op("V", ["pi"], ["pj"], lambda: V.tensor_scalar(T.pj[:, 0:1], T.pi[:, 0:1], 15, None, AluOpType.bitwise_and))
+    vts("mk", "m1", -1e29, None, mult, w=full)
+    vtt(full("dw"), ["dw"], full("wa"), ["wa"], full("m1"), ["m1"], add)
+    op("V", ["pj"], ["sc0"], lambda: V.tensor_scalar(T.sc0[:, 0:1], T.pj[:, 0:1], 15.0, 1.0 - 2.0 ** -16, eq, mult))
+    op("V", ["pj"], ["pf"], lambda: V.tensor_copy(T.pf[:, 0:1], T.pj[:, 0:1]))
+    op("V", ["uj"], ["uo"], lambda: V.tensor_copy(T.uo[:, 0:8], T.uj[:, 0:8]))
+    op("V", ["sc0"], ["sc1"], lambda: V.tensor_scalar(T.sc1[:, 0:1], T.sc0[:, 0:1], 2.0 ** -16, None, add))
+    vts("cw", "k16", T.pf[:, 0:1], None, add, extra=["pf"])
+    quant("ut", ["ut"], "uq", "uqs", 128)
+    op("V", ["uq", "uo"], ["uq2c"], lambda: V.tensor_copy(T.uq2[:, 0:128].bitcast(dt.uint32), T.uq[:, 0:128].bitcast(dt.uint32).indirect(T.uo[:, 0:8])))
+    op("A", ["uq", "uo"], ["uq2p"], lambda: A.activation(T.uq2s[:, 0:128], T.uqs[:, 0:128].indirect(T.uo[:, 0:8]), copy))
+    op("V", ["la32"], ["lz0"], lambda: V.tensor_copy(off("lz0"), off("la32")))
+    tiny("dz0", "lb32", "la32", sub)
+    units("e8", "c8", [0])
+
+    for k in range(ROUNDS):
+        dst, src = T.cores[(rank + STEP[k]) % 8], T.cores[(rank - STEP[k]) % 8]
+        xt, xq, xs, aq, asc, zq, zs, lz, dz = [n + str(k) for n in ("xt", "xq", "xs", "aq", "as", "zq", "zs", "lz", "dz")]
+        ta, tb, td, pt, pu, pv = [n + str(k) for n in ("ta", "tb", "td", "pt", "pu", "pv")]
+        nx, lz1, dz1 = [n + str(k + 1) for n in ("xt", "lz", "dz")]
+        last = k == ROUNDS - 1
+        lands(src, "rx%d" % k, [aq], 2)
+        lands(src, "ra%d" % k, [ta])
+        lands(src, "rb%d" % k, [tb])
+        lands(src, "rd%d" % k, [td])
+
+        xk = parts(xq)
+
+        def own():
+            for b in range(4):
+                mm(b, "c1", 128 * b, ["c1%d" % b], xq, xs, xk)
+
+        for h in (0, 1):
+            quant_half(xt, [xt] + [xt + "_%d" % b for b in range(4 + h)], xq, xs, h)
+            mm(4 + h, "uq2", 0, ["uq2c", "uq2p"], xq, xs, [xk[h]], *halves[h])
+        send(dst, "rx%d" % k, xk, full(aq).bitcast(dt.uint8), full(xq).bitcast(dt.uint8))
+        send(dst, "rx%d" % k, xk, full(asc), full(xs))
+        if k:
+            own()
+        else:
+            op("G", ["en"], ["e1"], lambda: g.affine_select(T.e1[:], T.en[:], [[1, 520]], eq, 0.0, -4, -4))
+            iota(T.alt[:], "alt", [[0, C], [1, 2]], 0, 0)
+            iota(T.fi[:], "fi", [[1, C]], 0, 0)
+        if k == 0:
+            wait_for("Y", [("dx", 16)])
+            dma("Y", "dwc", [], ["wqc"], T.wq[:].bitcast(dt.uint8), T.wc[:])
+            dma("Y", "dws", [], ["wqp"], T.wqs[:], T.ws[:])
+            dma("Y", "dv", [], ["vt"], T.vt[:], T.v[:])
+
+        if k == 0:
+            units("e8", "c8", [1])
+        for h in (0, 1):
+            vtt(full("bb", h), ["bb%d" % h], bank(4 + h, wide[h]), ["ps%d" % (4 + h)], full("mk", h), ["mk"], lt)
+        for h in (0, 1):
+            scan_part("m1", "bb", ["bb%d" % h], "se", h)
+        vtt(off("tm"), ["tm"], ends("se"), parts("se") + [], off(dz), [dz], mult)
+        tiny("pw", "tm", lz, add)
+        op("V", ["pw"], ["o0"], lambda: V.tensor_copy(off("o0"), off("pw")))
+        for h in (0, 1):
+            acopy(full("ssb", h), ["ssb%d" % h], bank(4 + h, wide[h]), ["ps%d" % (4 + h)])
+
+        op("V", ["ic", "o0"], ["t0b"], lambda: V.tensor_copy(full("t0", 1), full("ic").indirect(off("o0", 1))))
+        acopy(full("t0", 0), ["t0a"], full("ic").indirect(off("o0", 0)), ["ic", "o0"])
+        acopy(full("t1"), ["t1"], full("t0").indirect(off("o0")), ["t0a", "t0b", "o0"])
+        agather("t1", "o0", "t2")
+        low("ic", "o0", "ic2", "l0")
+        low("l0", "o0", "ic", "l1")
+        for h in (0, 1):
+            op("V", ["ps%d" % (4 + h)], ["ssc%d" % h], lambda: V.tensor_copy(full("ssc", h), bank(4 + h, wide[h])))
+        acopy(full("k1"), ["k1"], full("l1"), ["l1"])
+        for j in range(1, 7):
+            sn, o, t, l, m, kj, kn = "sc" if j % 2 else "sd", "o%d" % j, "t%d" % (j + 1), "l%d" % j, "l%d" % (j + 1), "k%d" % j, "k%d" % (j + 1)
+            tk, lk, kk = [(parts(n) if j > 1 else [n, n]) for n in (t, l, kj)]
+            for h in (0, 1):
+                scan_part("dw", t, [tk[h]], sn, h)
+            for h in (0, 1):
+                op("V", [parts(sn)[h], "sc1"], [parts(o)[h]], lambda: V.tensor_scalar(off(o, h), ends(sn, h), T.sc1[:, 0:1], 144.25, mult, add))
+            if j < 6:
+                for h in (0, 1):
+                    nt = "t%d" % (j + 2)
+                    acopy(full(nt, h), [parts(nt)[h]], full(t).indirect(off(o, h)), tk + [parts(o)[h]])
+            for h in (0, 1):
+                vtt(full(m, h), [parts(m)[h]], full(l).indirect(off(o, h)), lk + [parts(o)[h]], full(kj, h), [kk[h]], amin)
+            if j < 6:
+                for h in (0, 1):
+                    acopy(full(kn, h), [parts(kn)[h]], full(m, h), [parts(m)[h]])
+            if k == 0 and j in (2, 3):
+                units("e8", "c8", [j])
+        o6k = parts("o6")
+        tiny("cp", "cw", "pw", sub)
+        vtt(full("l8"), ["l8"], full("l7").indirect(off("o6")), parts("l7") + o6k, full("k6"), parts("k6"), amin)
+        op("V", ["cp", "sc1"], ["cs"], lambda: V.tensor_scalar(off("cs"), off("cp"), T.sc1[:, 0:1], None, mult))
+
+        for b in range(4):
+            mm(4 + b, "c8", 128 * b, ["c8%d" % b], aq, asc, [aq])
+        for b in range(3):
+            acopy(pl("z0", b), ["z0%d" % b], bank(4 + b), ["ps%d" % (4 + b)])
+
+        vtt(full("fl"), ["fl"], full("l8").indirect(off("o0")), ["l8", "o0"], full("ic"), ["ic"], eq)
+        vts("pq", "pw", 0.25, None, add)
+        scan("dw", "fl", "sa")
+        vtt(off("tn"), ["tn"], ends("sa"), ["sa"], off("cs"), ["cs"], mult)
+        tiny("tw", "tn", "pq", add)
+        op("V", ["tw"], [pt], lambda: V.tensor_copy(off(pt), off("tw")))
+        send(dst, "ra%d" % k, [pt], off(ta), off(pt))
+        acopy(full("rb"), ["rb"], full("l8").indirect(off("o6")), ["l8"] + o6k)
+        acopy(pl("z0", 3), ["z03"], bank(7), ["ps7"])
+
+        def vcast0(b):
+            op("V", ["ps%d" % (4 + b)], ["d0%d" % b], lambda: V.tensor_copy(pl("zd", b), bank(4 + b)))
+
+        def fcast(b):
+            acopy(pl("fo", b), ["fo%d" % b], bank(b), ["ps%d" % b])
+
+        agather("ic", pt, "q0")
+        agather("q0", pt, "q1")
+        for w, r in (("rb", "rc"), ("rc", "rd")):
+            op("V", [w] + o6k, [r], lambda: V.tensor_copy(full(r), full(w).indirect(off("o6"))))
+        vcast0(0)
+        scan("dw", "q1", "sb")
+        offsets("sb", pu)
+        send(dst, "rb%d" % k, [pu], off(tb), off(pu))
+        vcast0(1)
+        if k:
+            fcast(0)
+        agather("q1", pu, "q2")
+        if k:
+            fcast(1)
+            fcast(2)
+        scan("dw", "rd", "sa")
+        offsets("sa", "orr")
+        scan("dw", "q2", "sb")
+        offsets("sb", pv)
+        send(dst, "rd%d" % k, [pv], off(td), off(pv))
+        vtt(full("cm"), ["cm"], full("ssb").indirect(off("orr")), ["ssb0", "ssb1", "orr"], full("ssc"), ["ssc0", "ssc1"], gt)
+        scan("dw", "cm", "sa")
+        op("V", ["sa", "sc1"], ["xm"], lambda: V.tensor_scalar(off("xm"), ends("sa"), T.sc1[:, 0:1], 0.5, mult, gt))
+        if k == 0:
+            units("e1", "c1")
+            own()
+
+        def step(i, b, o):
+            x, out = "z%d" % (i - 1), (el("z3", b) if i == 3 else pl("z%d" % i, b))
+            n = 2 * (i - 1) + b
+            vtt(out, ["z%d%d" % (i, b)], pl(x, b).indirect(off(o)), [x + str(b), o], pl("zd", n), ["d%d%d" % (i - 1, b)], add)
+
+        def twin(i, b):
+            n = 2 * i + b
+            op("V", ["z%d%d" % (i, b)], ["d%d%d" % (i, b)], lambda: V.tensor_copy(pl("zd", n), pl("z%d" % i, b)))
+
+        def stream(i, b):
+            n = {1: 0, 2: 4, 3: 8}[i] + 2 * (b - 2)
+            return n * C, (n + 2) * C
+
+        def stage(i, b, o):
+            a, e = stream(i, b)
+            s, z = stream(1, b)
+            win, one, xk = (T.st[:, s:z], T.st[:, s + 1:z:2], "u%d" % b) if i == 3 else (pl("z1", b), pl("z1", b), "z1%d" % b)
+            acopy(T.st[:, a + 1:e:2], ["y%d%d" % (i, b)], one, [xk])
+            acopy(T.st[:, a:e:2], ["w%d%d" % (i, b)], win.indirect(off(o)), [xk, o])
+
+        def pairs(i, b):
+            a, e = stream(i, b)
+            s, z = stream(1, b)
+            out, ok = (T.z3[:, b - 2:4 * C:2], ["z3%d" % b, "z3%d" % (b - 2)]) if i == 3 else (T.st[:, s:z], ["u%d" % b])
+            op("V", ["alt", "y%d%d" % (i, b), "w%d%d" % (i, b)], ok, lambda: V.tensor_tensor_scan(out, T.alt[:], T.st[:, a:e], 0.0, mult, add))
+
+        def half(b):
+            vtt(pl("z1", b), ["z1%d" % b], pl("gb", b - 2), ["gb%d" % b], bank(4 + b), ["ps%d" % (4 + b)], add)
+
+        for b in (2, 3):
+            acopy(pl("gb", b - 2), ["gb%d" % b], pl("z0", b).indirect(off(ta)), ["z0%d" % b, ta])
+        step(1, 0, ta)
+        tiny("xd", "xm", dz, mult)
+        half(2)
+        stage(2, 2, tb)
+        twin(1, 0)
+        step(1, 1, ta)
+        half(3)
+        stage(2, 3, tb)
+        twin(1, 1)
+        step(2, 0, tb)
+        pairs(2, 2)
+        twin(2, 0)
+        op("V", [td], ["te"], lambda: V.tensor_scalar(off("te"), off(td), 2.0, 1.0, mult, add))
+        stage(3, 2, "te")
+        step(2, 1, tb)
+        pairs(2, 3)
+        stage(3, 3, "te")
+        if k == 0:
+            for b in range(3):
+                fcast(b)
+        twin(2, 1)
+        pairs(3, 2)
+        vts("xe", "xm", -2.0, 1.0, mult, add)
+        step(3, 0, td)
+        pairs(3, 3)
+        if k == 0:
+            quant("vt", ["vt"], "vq", "vqs", 128)
+        for h, (a, e) in enumerate(halves):
+            vtt(T.z3[:, 4 * a + 1:4 * e:4], ["z31" + "ab"[h]], pl("z2", 1).indirect(off(td, h)), ["z21", "z31", td], T.zd[:, 5 * C + a:5 * C + e], ["d21"], add)
+        zk = parts(zq)
+        for h in (0, 1):
+            quant_half("z3", ["z30", "z31", "z32", "z33"] + parts("z31")[0:h + 1], zq, zs, h)
+            mm(h, "wq", 0, ["wqc", "wqp"], zq, zs, [zk[h]], *halves[h])
+
+        tiny(lz1, lz, "xd", add)
+        tiny(dz1, dz, "xe", mult)
+        if last:
+            op("V", [lz1], ["loa"], lambda: V.tensor_copy(T.lo[:, 0:K], off(lz1)))
+            tiny("l1f", lz1, dz1, add)
+            op("V", ["l1f"], ["lob"], lambda: V.tensor_copy(T.lo[:, K:2 * K], off("l1f")))
+
+        for b in (1, 3, 2):
+            mm(4 + b, "wq", 128 * b, ["wqc", "wqp"], zq, zs, zk)
+        op("V", ["ps0"], ["hb0a"], lambda: V.tensor_scalar(T.hb[:, 0:CUT], bank(0, CUT), 0.03125, None, mult))
+        acopy(T.hb[:, CUT:C], ["hb0b"], bank(1, C - CUT), ["ps1"], 0.03125)
+        for b in (1, 3, 2):
+            acopy(pl("hb", b), ["hb%d" % b], bank(4 + b), ["ps%d" % (4 + b)], 0.03125)
+        acopy(full("xg"), ["xg"], pl("hb", 3).indirect(off(pt)), ["hb3", pt])
+        for b in range(3):
+            vtt(el(nx, b), [nx + "_%d" % b], pl("hb", b).indirect(off(pt)), ([] if b else ["hb0a", "hb0b"]) + ["hb%d" % b, pt], pl("fo", b), ["fo%d" % b], add)
+        for h, (a, e) in enumerate(halves):
+            vtt(T[nx][:, 4 * a + 3:4 * e:4], [nx + "_%d" % (3 + h)], T.xg[:, a:e], ["xg"], T.ps3[:, a:e], ["ps3"], add)
+        if last:
+            acopy(T.lrep[:], ["lrep"], full("fi").indirect(T.lo[:, 0:2 * K]), ["fi", "loa", "lob"])
+            dma("Y", "dls", ["lrep"], [], T.ls[:], T.lrep[0:128:16, :])
+
+    xq, xs = "xq%d" % ROUNDS, "xs%d" % ROUNDS
+    xk = parts(xq)
+    for h in (0, 1):
+        quant_half("xt%d" % ROUNDS, ["xt%d_%d" % (ROUNDS, b) for b in range(4 + h)], xq, xs, h)
+        mm(h, "vq", 0, ["vq"], xq, xs, [xk[h]], *halves[h])
+    dma("Y", "doc", xk, [], T.oc[:], full(xq).bitcast(dt.uint8))
+    for i in range(4):
+        dma("Y", "dsc%d" % i, xk, [], T.osc[4 * i:4 * i + 4, :], T[xs][32 * i:32 * i + 4, :])
+    acopy(T.yo[:, 0:CUT], ["yo0"], bank(0, CUT), ["ps0"])
+    op("V", ["ps1"], ["yo1"], lambda: V.tensor_copy(T.yo[:, CUT:C], bank(1, C - CUT)))
+    dma("A", "dy0", ["yo0"], [], T.y[:, 0:CUT], T.yo[:, 0:CUT])
+    dma("Y", "dy1", ["yo1"], [], T.y[:, CUT:C], T.yo[:, CUT:C])
+    for s in total:
+        if known["Y"].get(s, 0) < total[s]:
+            Q["Y"].wait_ge(T.sem[s], total[s])

@@ -6,6 +6,9 @@ STEP = [4, 1, 2]
 ROUNDS = len(STEP)
 HALF = C // 2
 CUT = 160
+WHOLE = 1024.0
+
+ORDER = "Lw Da Db sa sb ta pa tb pb ma mb"
 
 SCRATCH = {}
 
@@ -23,18 +26,20 @@ def _declare():
             s[n + str(k)] = ("sbuf", [128, 32], "uint16")
         s["zq%d" % k] = ("sbuf", [128, C], "float8_e4m3fn_x4")
         s["zs%d" % k] = ("sbuf", [128, C], "uint8")
-    for n, w in (("ut", 512), ("vt", 512), ("em", 520), ("en", 520), ("e1", 520), ("e8", 520), ("ic", C), ("m1", C), ("mk", C),
-                 ("dw", C), ("bb", C), ("sa", C), ("sb", C), ("sc", C), ("sd", C), ("se", C), ("fl", C), ("cm", C), ("rb", C), ("rc", C), ("rd", C),
-                 ("q0", C), ("q1", C), ("q2", C), ("xg", C), ("alt", 2 * C), ("st", 12 * C), ("tab", 24 * C), ("ic2", C), ("zd", 6 * C),
-                 ("fo", 4 * C), ("z0", 4 * C), ("z1", 4 * C), ("z2", 4 * C), ("z3", 4 * C), ("gb", 2 * C), ("hb", 4 * C)):
+    for n, w in (("ut", 512), ("vt", 512), ("em", 520), ("en", 2 * C), ("e1", 520), ("e8", 520), ("ic", C), ("mk", C),
+                 ("dw", C), ("sa", C), ("sb", C), ("sc", C), ("sd", C), ("cm", C), ("l2s", C),
+                 ("q0", C), ("q1", C), ("q2", C), ("xg", C), ("tab", 24 * C), ("zd", 6 * C),
+                 ("fo", 4 * C), ("z0", 4 * C), ("z1", 4 * C), ("z2", 4 * C), ("z3", 4 * C), ("gb", 8 * C), ("hb", 4 * C)):
         s[n] = ("sbuf", [128, w], "bfloat16")
+    for n, w in (("sg", 2 * C), ("sw", 2 * C), ("sp", 2 * C), ("tz", 64), ("tp", 64), ("to", 64), ("le", 24)):
+        s[n] = ("sbuf", [128, w], "float16")
     for n, w in (("ol", 32 * 9), ("snt", 32 * 3 * ROUNDS), ("uo", 32)):
         s[n] = ("sbuf", [128, w], "uint16")
     s["lo"] = ("sbuf", [128, 64], "uint16")
     for n, w in (("ri", C), ("rr", C), ("pi", 8), ("pj", 8), ("k16", 24), ("uj", 8), ("la32", 24), ("lb32", 24)):
         s[n] = ("sbuf", [128, w], "int32")
-    for n, w in (("wa", C), ("ssb", C), ("ssc", C), ("fi", C), ("lrep", 2 * C), ("yo", C), ("sc0", 8), ("sc1", 8), ("pf", 8), ("cw", 24), ("tm", 24), ("pw", 24),
-                 ("cp", 24), ("cs", 24), ("pq", 24), ("tn", 24), ("tw", 24), ("xm", 24), ("xd", 24), ("xe", 24), ("l1f", 24), ("lst", 32 * 8)):
+    for n, w in (("wa", C), ("m1", C), ("ssb", C), ("sl1", C), ("sl2", C), ("sl3", C), ("fi", C), ("lrep", 2 * C), ("yo", C), ("sc0", 8), ("sc1", 8), ("thr", 8),
+                 ("pf", 8), ("cw", 24), ("cv", 24), ("xe", 24), ("sm", 24), ("hd", 24), ("l0f", 24), ("l1f", 24)):
         s[n] = ("sbuf", [128, w], "float32")
     for n, w in (("uq", 128), ("uq2", 128), ("vq", 128), ("wq", 512), ("c1", 512), ("c8", 512)):
         s[n] = ("sbuf", [128, w], "float8_e4m3fn_x4")
@@ -115,13 +120,14 @@ def rank_program(g, core, T, topo):
             readers[b] = []
 
     V, A, P = g.vector, g.scalar, g.tensor
-    mult, add, sub, lt, gt, eq, amin = (AluOpType.mult, AluOpType.add, AluOpType.subtract, AluOpType.is_lt, AluOpType.is_gt, AluOpType.is_equal, AluOpType.min)
-    copy = ActivationFunctionType.Copy
+    mult, add, sub, lt, gt, eq, ne, amin = (AluOpType.mult, AluOpType.add, AluOpType.subtract, AluOpType.is_lt, AluOpType.is_gt, AluOpType.is_equal,
+                                            AluOpType.not_equal, AluOpType.min)
+    copy, sign = ActivationFunctionType.Copy, ActivationFunctionType.Sign
     tables = {n: i * C for i, n in enumerate(["t%d" % i for i in range(9)] + ["l%d" % i for i in range(9)] + ["k%d" % i for i in range(1, 7)])}
-    lists = {n: i * 32 for i, n in enumerate(["lz%d" % i for i in range(ROUNDS + 1)] + ["dz%d" % i for i in range(ROUNDS + 1)])}
 
     halves = ((0, CUT), (CUT, C))
     wide = (CUT, C - CUT)
+    runs = ((0, CUT // 16), (CUT // 16, K))
 
     def parts(n):
         return [n + "a", n + "b"]
@@ -132,26 +138,24 @@ def rank_program(g, core, T, topo):
             return T.tab[:, tables[n] + a:tables[n] + e]
         return T[n][:, a:e]
 
-    picks = {n: i * 32 for i, n in enumerate(["o%d" % i for i in range(7)] + ["orr", "te"])}
+    picks = {n: i * 32 for i, n in enumerate(["o%d" % i for i in range(9)])}
     sent = {n + str(i): (3 * i + j) * 32 for i in range(ROUNDS) for j, n in enumerate(["pt", "pu", "pv"])}
 
     def off(n, h=None):
+        a, e = (0, K) if h is None else runs[h]
         if n in picks:
-            a, e = (0, K) if h is None else (halves[h][0] // 16, halves[h][1] // 16)
             return T.ol[:, picks[n] + a:picks[n] + e]
-        if h is not None:
-            return T[n][:, halves[h][0] // 16:halves[h][1] // 16]
         if n in sent:
-            return T.snt[:, sent[n]:sent[n] + K]
-        if n in lists:
-            return T.lst[:, lists[n]:lists[n] + K]
-        return T[n][:, 0:K]
+            return T.snt[:, sent[n] + a:sent[n] + e]
+        return T[n][:, a:e]
 
-    def pl(n, b):
-        return T[n][:, b * C:(b + 1) * C]
+    def pl(n, b, h=None):
+        a, e = (0, C) if h is None else halves[h]
+        return T[n][:, b * C + a:b * C + e]
 
-    def el(n, b):
-        return T[n][:, b:4 * C:4]
+    def el(n, b, h=None):
+        a, e = (0, C) if h is None else halves[h]
+        return T[n][:, 4 * a + b:4 * e:4]
 
     def ends(n, h=None):
         a, e = (0, C) if h is None else halves[h]
@@ -163,38 +167,28 @@ def rank_program(g, core, T, topo):
     def vtt(out, ok, a, ak, b, bk, o):
         op("V", ak + bk, ok, lambda: V.tensor_tensor(out, a, b, o))
 
-    def vts(out, a, s1, s2, o1, *o2, w=off, extra=()):
-        op("V", [a] + list(extra), [out], lambda: V.tensor_scalar(w(out), w(a), s1, s2, o1, *o2))
+    def vts(out, ok, a, ak, s1, s2, *o):
+        op("V", ak, ok, lambda: V.tensor_scalar(out, a, s1, s2, *o))
 
-    def scan(d0, d1, out):
-        op("V", [d0, d1], [out], lambda: V.tensor_tensor_scan(full(out), full(d0), full(d1), 0.0, mult, add))
+    def vcopy(out, ok, in_, ik):
+        op("V", ik, ok, lambda: V.tensor_copy(out, in_))
 
-    def offsets(sc, out):
-        op("V", [sc, "sc1"], [out], lambda: V.tensor_scalar(off(out), ends(sc), T.sc1[:, 0:1], 144.25, mult, add))
+    def vscan(out, ok, d0, d1, ik):
+        op("V", ik, ok, lambda: V.tensor_tensor_scan(out, d0, d1, 0.0, mult, add))
 
     def acopy(out, ok, in_, ik, scale=1.0):
         op("A", ik, ok, lambda: A.activation(out, in_, copy, scale=scale))
 
-    def agather(win, o, out):
-        acopy(full(out), [out], full(win).indirect(off(o)), [win, o])
+    def wrap(src, sk, sn, out, ok):
+        vscan(full(sn), [sn], full("dw"), full(src), ["dw"] + sk)
+        vts(off(out), ok, ends(sn), [sn, "sc1"], T.sc1[:, 0:1], 144.25, mult, add)
 
-    def vgather(win, o, out):
-        op("V", [win, o], [out], lambda: V.tensor_copy(full(out), full(win).indirect(off(o))))
-
-    def low(win, o, other, out):
-        vtt(full(out), [out], full(win).indirect(off(o)), [win, o], full(other), [other], amin)
-
-    def again(src, out):
-        op("V", [src], [out], lambda: V.tensor_copy(full(out), full(src)))
-
-    def tiny(out, a, b, o):
-        vtt(off(out), [out], off(a), [a], off(b), [b], o)
+    def shared(win, wk, o, ok, out):
+        acopy(full(out, 0), [parts(out)[0]], full(win).indirect(off(o, 0)), wk + ok)
+        vcopy(full(out, 1), [parts(out)[1]], full(win).indirect(off(o, 1)), wk + ok)
 
     def quant(t, tk, q, s, w=C):
         op("V", tk, [q], lambda: V.quantize_mx(T[q][:, 0:w], T[s][:, 0:w], T[t][:, 0:4 * w]))
-
-    def scan_part(d0, src, sk, out, h):
-        op("V", [d0] + sk, [parts(out)[h]], lambda: V.tensor_tensor_scan(full(out, h), full(d0, h), full(src, h), 0.0, mult, add))
 
     def quant_half(t, tk, q, s, h):
         a, e = halves[h]
@@ -212,43 +206,57 @@ def rank_program(g, core, T, topo):
     def iota(out, ok, pattern, base, cm):
         op("G", [], [ok], lambda: g.iota(out, pattern, base, cm, allow_small_or_imprecise_dtypes=True))
 
+    def fill(out, ok, x):
+        op("V", [], ok, lambda: V.memset(out, x))
+
     dma("Y", "dx", [], ["xt0"], T.xt0[:], T.x[:])
     dma("A", "du", [], ["ut"], T.ut[:], T.u[:])
     dma("Y", "dla", [], ["la32"], off("la32"), T.la[:])
     dma("A", "dlb", [], ["lb32"], off("lb32"), T.lb[:])
-    op("V", [], ["em"], lambda: V.memset(T.em[:], 0.125))
-    op("V", [], ["en"], lambda: V.memset(T.en[:], 1.0))
+    fill(T.em[:], ["em"], 0.125)
+    fill(T.en[:], ["en"], 1.0)
     iota(T.ri[:], "ri", [[-1, C]], C, 1)
     iota(T.pi[:, 0:1], "pi", [[0, 1]], 0, 1)
     iota(T.uj[:, 0:8], "uj", [[16, 8]], 0, 0)
     iota(off("k16"), "k16", [[16, K]], 0, 0)
-    op("G", ["em"], ["e8"], lambda: g.affine_select(T.e8[:], T.em[:], [[1, 520]], eq, 0.0, -4, -4))
     iota(T.ic[:], "ic", [[1, C]], -HALF, 0)
-    iota(T.ic2[:], "ic2", [[1, C]], -HALF, 0)
+    op("G", ["em"], ["e8"], lambda: g.affine_select(T.e8[:], T.em[:], [[1, 520]], eq, 0.0, -4, -4))
 
-    vts("rr", "ri", 15, None, AluOpType.bitwise_and, w=full)
-    vts("m1", "rr", 1.0, None, amin, w=full)
-    vts("wa", "rr", 15.0, 65535.0, eq, mult, w=full)
-    op("V", ["pi"], ["pj"], lambda: V.tensor_scalar(T.pj[:, 0:1], T.pi[:, 0:1], 15, None, AluOpType.bitwise_and))
-    vts("mk", "m1", -1e29, None, mult, w=full)
+    s1 = T.sc1[:, 0:1]
+    vts(full("rr"), ["rr"], full("ri"), ["ri"], 15, None, AluOpType.bitwise_and)
+    vts(T.pj[:, 0:1], ["pj"], T.pi[:, 0:1], ["pi"], 15, None, AluOpType.bitwise_and)
+    vcopy(T.uo[:, 0:8], ["uo"], T.uj[:, 0:8], ["uj"])
+    vts(full("m1"), ["m1"], full("rr"), ["rr"], 1.0, None, amin)
+    vts(full("wa"), ["wa"], full("rr"), ["rr"], 15.0, 65535.0, eq, mult)
+    vts(T.sc0[:, 0:1], ["sc0"], T.pj[:, 0:1], ["pj"], 15.0, 1.0 - 2.0 ** -16, eq, mult)
+    vcopy(T.pf[:, 0:1], ["pf"], T.pj[:, 0:1], ["pj"])
+    vts(full("mk"), ["mk"], full("m1"), ["m1"], -1e29, None, mult)
+    vcopy(T.sw[:], ["sw", "dz"], T.en[:], ["en"])
+    vts(T.sg[:], ["sg", "sg0", "sg1", "mid"], T.en[:], ["en"], 0.0, None, mult)
     vtt(full("dw"), ["dw"], full("wa"), ["wa"], full("m1"), ["m1"], add)
-    op("V", ["pj"], ["sc0"], lambda: V.tensor_scalar(T.sc0[:, 0:1], T.pj[:, 0:1], 15.0, 1.0 - 2.0 ** -16, eq, mult))
-    op("V", ["pj"], ["pf"], lambda: V.tensor_copy(T.pf[:, 0:1], T.pj[:, 0:1]))
-    op("V", ["uj"], ["uo"], lambda: V.tensor_copy(T.uo[:, 0:8], T.uj[:, 0:8]))
-    op("V", ["sc0"], ["sc1"], lambda: V.tensor_scalar(T.sc1[:, 0:1], T.sc0[:, 0:1], 2.0 ** -16, None, add))
-    vts("cw", "k16", T.pf[:, 0:1], None, add, extra=["pf"])
+    vts(s1, ["sc1"], T.sc0[:, 0:1], ["sc0"], 2.0 ** -16, None, add)
+    vts(off("cw"), ["cw"], off("k16"), ["k16", "pf"], T.pf[:, 0:1], None, add)
+    vts(T.sw[:, 0:2 * C:32], ["sw"], off("k16"), ["k16"], 0.0, None, mult)
+    vts(T.sg[:, 1:2 * C:32], ["sg"], off("k16"), ["k16"], 0.0, -0.5, mult, add)
+    dz, mid, chosen = T.sw[:, 31:2 * C:32], T.sg[:, 31:2 * C:32], T.sp[:, 31:2 * C:32]
     quant("ut", ["ut"], "uq", "uqs", 128)
-    op("V", ["uq", "uo"], ["uq2c"], lambda: V.tensor_copy(T.uq2[:, 0:128].bitcast(dt.uint32), T.uq[:, 0:128].bitcast(dt.uint32).indirect(T.uo[:, 0:8])))
+    vcopy(T.uq2[:, 0:128].bitcast(dt.uint32), ["uq2c"], T.uq[:, 0:128].bitcast(dt.uint32).indirect(T.uo[:, 0:8]), ["uq", "uo"])
     op("A", ["uq", "uo"], ["uq2p"], lambda: A.activation(T.uq2s[:, 0:128], T.uqs[:, 0:128].indirect(T.uo[:, 0:8]), copy))
-    op("V", ["la32"], ["lz0"], lambda: V.tensor_copy(off("lz0"), off("la32")))
-    tiny("dz0", "lb32", "la32", sub)
-    units("e8", "c8", [0])
+
+    def late_constants():
+        vts(T.thr[:, 0:1], ["thr"], T.pj[:, 0:1], ["pj"], 15.0, 0.5 - 2.0 ** 15, eq, mult)
+        vts(T.tz[:, 0:3 * K:3], ["tz0"], off("k16"), ["k16"], 0.0, None, mult)
+        vts(T.tz[:, 1:3 * K:3], ["tz1"], off("k16"), ["k16"], 0.0, 1.0, mult, add)
+        vts(T.thr[:, 0:1], ["thr"], T.thr[:, 0:1], ["thr"], 2.0 ** 15, None, add)
+        vts(T.tp[:, 1:3 * K:3], ["tp1"], off("cw"), ["cw"], -1.0, None, mult)
+        vcopy(T.tp[:, 2:3 * K:3], ["tp2"], off("cw"), ["cw"])
+        vts(off("cv"), ["cv"], off("cw"), ["cw"], WHOLE, None, add)
 
     for k in range(ROUNDS):
         dst, src = T.cores[(rank + STEP[k]) % 8], T.cores[(rank - STEP[k]) % 8]
-        xt, xq, xs, aq, asc, zq, zs, lz, dz = [n + str(k) for n in ("xt", "xq", "xs", "aq", "as", "zq", "zs", "lz", "dz")]
+        xt, xq, xs, aq, asc, zq, zs = [n + str(k) for n in ("xt", "xq", "xs", "aq", "as", "zq", "zs")]
         ta, tb, td, pt, pu, pv = [n + str(k) for n in ("ta", "tb", "td", "pt", "pu", "pv")]
-        nx, lz1, dz1 = [n + str(k + 1) for n in ("xt", "lz", "dz")]
+        nx = "xt%d" % (k + 1)
         last = k == ROUNDS - 1
         lands(src, "rx%d" % k, [aq], 2)
         lands(src, "ra%d" % k, [ta])
@@ -261,6 +269,9 @@ def rank_program(g, core, T, topo):
             for b in range(4):
                 mm(b, "c1", 128 * b, ["c1%d" % b], xq, xs, xk)
 
+        def fcast(b):
+            acopy(pl("fo", b), ["fo%d" % b], bank(b), ["ps%d" % b])
+
         for h in (0, 1):
             quant_half(xt, [xt] + [xt + "_%d" % b for b in range(4 + h)], xq, xs, h)
             mm(4 + h, "uq2", 0, ["uq2c", "uq2p"], xq, xs, [xk[h]], *halves[h])
@@ -269,206 +280,182 @@ def rank_program(g, core, T, topo):
         if k:
             own()
         else:
-            op("G", ["en"], ["e1"], lambda: g.affine_select(T.e1[:], T.en[:], [[1, 520]], eq, 0.0, -4, -4))
-            iota(T.alt[:], "alt", [[0, C], [1, 2]], 0, 0)
+            op("G", ["en"], ["e1"], lambda: g.affine_select(T.e1[:], T.en[:, 0:520], [[1, 520]], eq, 0.0, -4, -4))
             iota(T.fi[:], "fi", [[1, C]], 0, 0)
-        if k == 0:
             wait_for("Y", [("dx", 16)])
             dma("Y", "dwc", [], ["wqc"], T.wq[:].bitcast(dt.uint8), T.wc[:])
             dma("Y", "dws", [], ["wqp"], T.wqs[:], T.ws[:])
             dma("Y", "dv", [], ["vt"], T.vt[:], T.v[:])
+            vtt(off("sm"), ["sm"], off("la32"), ["la32"], off("lb32"), ["lb32"], add)
+            vtt(dz, ["dz"], off("lb32"), ["lb32"], off("la32"), ["la32"], sub)
+            vts(mid, ["mid"], off("sm"), ["sm"], 0.5, None, mult)
 
-        if k == 0:
-            units("e8", "c8", [1])
-        for h in (0, 1):
-            vtt(full("bb", h), ["bb%d" % h], bank(4 + h, wide[h]), ["ps%d" % (4 + h)], full("mk", h), ["mk"], lt)
-        for h in (0, 1):
-            scan_part("m1", "bb", ["bb%d" % h], "se", h)
-        vtt(off("tm"), ["tm"], ends("se"), parts("se") + [], off(dz), [dz], mult)
-        tiny("pw", "tm", lz, add)
-        op("V", ["pw"], ["o0"], lambda: V.tensor_copy(off("o0"), off("pw")))
+        for h, (a, e) in enumerate(halves):
+            vtt(T.sg[:, 2 * a:2 * e:2], ["sg%d" % h], bank(4 + h, wide[h]), ["ps%d" % (4 + h)], full("mk", h), ["mk"], lt)
+        for h, (a, e) in enumerate(halves):
+            vscan(T.sp[:, 2 * a:2 * e], [parts("sp")[h]], T.sw[:, 2 * a:2 * e], T.sg[:, 2 * a:2 * e], ["sw", "dz", "sg", "sg%d" % h, "mid"])
+        for h, (a, e) in enumerate(halves):
+            vcopy(off("o0", h), [parts("o0")[h]], T.sp[:, 2 * a + 31:2 * e:32], [parts("sp")[h]])
         for h in (0, 1):
             acopy(full("ssb", h), ["ssb%d" % h], bank(4 + h, wide[h]), ["ps%d" % (4 + h)])
 
-        op("V", ["ic", "o0"], ["t0b"], lambda: V.tensor_copy(full("t0", 1), full("ic").indirect(off("o0", 1))))
-        acopy(full("t0", 0), ["t0a"], full("ic").indirect(off("o0", 0)), ["ic", "o0"])
-        acopy(full("t1"), ["t1"], full("t0").indirect(off("o0")), ["t0a", "t0b", "o0"])
-        agather("t1", "o0", "t2")
-        low("ic", "o0", "ic2", "l0")
-        low("l0", "o0", "ic", "l1")
-        for h in (0, 1):
-            op("V", ["ps%d" % (4 + h)], ["ssc%d" % h], lambda: V.tensor_copy(full("ssc", h), bank(4 + h, wide[h])))
-        acopy(full("k1"), ["k1"], full("l1"), ["l1"])
-        for j in range(1, 7):
-            sn, o, t, l, m, kj, kn = "sc" if j % 2 else "sd", "o%d" % j, "t%d" % (j + 1), "l%d" % j, "l%d" % (j + 1), "k%d" % j, "k%d" % (j + 1)
-            tk, lk, kk = [(parts(n) if j > 1 else [n, n]) for n in (t, l, kj)]
-            for h in (0, 1):
-                scan_part("dw", t, [tk[h]], sn, h)
-            for h in (0, 1):
-                op("V", [parts(sn)[h], "sc1"], [parts(o)[h]], lambda: V.tensor_scalar(off(o, h), ends(sn, h), T.sc1[:, 0:1], 144.25, mult, add))
-            if j < 6:
-                for h in (0, 1):
-                    nt = "t%d" % (j + 2)
-                    acopy(full(nt, h), [parts(nt)[h]], full(t).indirect(off(o, h)), tk + [parts(o)[h]])
-            for h in (0, 1):
-                vtt(full(m, h), [parts(m)[h]], full(l).indirect(off(o, h)), lk + [parts(o)[h]], full(kj, h), [kk[h]], amin)
-            if j < 6:
-                for h in (0, 1):
-                    acopy(full(kn, h), [parts(kn)[h]], full(m, h), [parts(m)[h]])
-            if k == 0 and j in (2, 3):
-                units("e8", "c8", [j])
+        acopy(full("t0", 0), ["t0a"], full("ic").indirect(off("o0", 0)), ["ic", "o0a"])
+        vcopy(T.tp[:, 0:3 * K:3], ["tp0"], chosen, parts("sp"))
+        vcopy(full("t0", 1), ["t0b"], full("ic").indirect(off("o0", 1)), ["ic", "o0b"])
+        shared("t0", parts("t0"), "o0", parts("o0"), "t1")
+        shared("t1", parts("t1"), "o0", parts("o0"), "t2")
+        vtt(full("l2s"), ["l2s"], full("t0"), parts("t0"), full("t1"), parts("t1"), amin)
+        def level(c, j):
+            h = "ab".index(c[1]) if c[1] != "w" else None
+            sn, o, t, nt, l, m, kj = "sc" if j % 2 else "sd", "o%d" % j, "t%d" % (j + 1), "t%d" % (j + 2), "l%d" % j, "l%d" % (j + 1), "k%d" % j
+
+            def key(n):
+                return parts(n) if h is None else [parts(n)[h]]
+
+            if j < 1 or j > 6:
+                return
+            if c[0] == "s":
+                vscan(full(sn, h), key(sn), full("dw", h), full(t, h), ["dw"] + key(t))
+            if c[0] == "t":
+                vts(off(o, h), key(o), ends(sn, h), key(sn) + ["sc1"], s1, 144.25, mult, add)
+            if c[0] == "p" and j < 6:
+                acopy(full(nt, h), key(nt), full(t).indirect(off(o, h)), parts(t) + key(o))
+            if c[0] == "m":
+                vtt(full(m, h), key(m), full(l).indirect(off(o, h)), parts(l) + key(o), full(kj, h), key(kj), amin)
+            if c[0] == "d":
+                vcopy(full(kj, h), key(kj), full(l, h), key(l))
+            if c[0] == "D":
+                acopy(full(kj, h), key(kj), full(l, h), key(l))
+            if c[0] == "L" and j == 1:
+                vtt(full(l), parts(l), full("l2s"), ["l2s"], full("t2"), parts("t2"), amin)
+
+        for j in range(1, 8):
+            for c in ORDER.split():
+                level(c, j - (int(c[2]) if len(c) > 2 else 0))
+            if k == 0 and j < 5:
+                units("e8", "c8", [j - 1])
+            if k == 0 and j == 5:
+                late_constants()
         o6k = parts("o6")
-        tiny("cp", "cw", "pw", sub)
-        vtt(full("l8"), ["l8"], full("l7").indirect(off("o6")), parts("l7") + o6k, full("k6"), parts("k6"), amin)
-        op("V", ["cp", "sc1"], ["cs"], lambda: V.tensor_scalar(off("cs"), off("cp"), T.sc1[:, 0:1], None, mult))
+        vtt(full("l8"), ["l8"], full("l7").indirect(off("o6")), parts("l7") + o6k, full("l6"), parts("l6"), amin)
 
         for b in range(4):
             mm(4 + b, "c8", 128 * b, ["c8%d" % b], aq, asc, [aq])
-        for b in range(3):
+        for b in range(4):
             acopy(pl("z0", b), ["z0%d" % b], bank(4 + b), ["ps%d" % (4 + b)])
+        if k:
+            for b in range(2):
+                fcast(b)
 
-        vtt(full("fl"), ["fl"], full("l8").indirect(off("o0")), ["l8", "o0"], full("ic"), ["ic"], eq)
-        vts("pq", "pw", 0.25, None, add)
-        scan("dw", "fl", "sa")
-        vtt(off("tn"), ["tn"], ends("sa"), ["sa"], off("cs"), ["cs"], mult)
-        tiny("tw", "tn", "pq", add)
-        op("V", ["tw"], [pt], lambda: V.tensor_copy(off(pt), off("tw")))
+        vscan(full("sa"), ["sa"], full("dw"), full("l8"), ["dw", "l8"])
+        vts(off("le"), ["le"], ends("sa"), ["sa", "sc1"], s1, WHOLE + HALF, mult, add)
+        vts(off("o8"), ["o8"], ends("sa"), ["sa", "sc1"], s1, 144.25, mult, add)
+        vtt(T.tz[:, 2:3 * K:3], ["tz2"], off("le"), ["le"], off("cv"), ["cv"], ne)
+        vscan(T.to[:, 0:3 * K], ["to"], T.tz[:, 0:3 * K], T.tp[:, 0:3 * K], ["tz0", "tz1", "tz2", "tp0", "tp1", "tp2"])
+        vcopy(off(pt), [pt], T.to[:, 2:3 * K:3], ["to"])
         send(dst, "ra%d" % k, [pt], off(ta), off(pt))
-        acopy(full("rb"), ["rb"], full("l8").indirect(off("o6")), ["l8"] + o6k)
-        acopy(pl("z0", 3), ["z03"], bank(7), ["ps7"])
 
-        def vcast0(b):
-            op("V", ["ps%d" % (4 + b)], ["d0%d" % b], lambda: V.tensor_copy(pl("zd", b), bank(4 + b)))
+        def twin(i, b):
+            vcopy(pl("zd", 2 * i + b), ["d%d%d" % (i, b)], pl("z%d" % i, b), ["z%d%d" % (i, b)])
 
-        def fcast(b):
-            acopy(pl("fo", b), ["fo%d" % b], bank(b), ["ps%d" % b])
-
-        agather("ic", pt, "q0")
-        agather("q0", pt, "q1")
-        for w, r in (("rb", "rc"), ("rc", "rd")):
-            op("V", [w] + o6k, [r], lambda: V.tensor_copy(full(r), full(w).indirect(off("o6"))))
-        vcast0(0)
-        scan("dw", "q1", "sb")
-        offsets("sb", pu)
+        twin(0, 1)
+        shared("ic", ["ic"], pt, [pt], "q0")
+        shared("q0", parts("q0"), pt, [pt], "q1")
+        acopy(full("sl1"), ["sl1"], full("ssb").indirect(off("o8")), ["ssb0", "ssb1", "o8"])
+        wrap("q1", parts("q1"), "sb", pu, [pu])
         send(dst, "rb%d" % k, [pu], off(tb), off(pu))
-        vcast0(1)
-        if k:
-            fcast(0)
-        agather("q1", pu, "q2")
-        if k:
-            fcast(1)
-            fcast(2)
-        scan("dw", "rd", "sa")
-        offsets("sa", "orr")
-        scan("dw", "q2", "sb")
-        offsets("sb", pv)
+        twin(0, 0)
+        shared("q1", parts("q1"), pu, [pu], "q2")
+        acopy(full("sl2"), ["sl2"], full("sl1").indirect(off("o6")), ["sl1"] + o6k)
+        wrap("q2", parts("q2"), "sa", pv, [pv])
         send(dst, "rd%d" % k, [pv], off(td), off(pv))
-        vtt(full("cm"), ["cm"], full("ssb").indirect(off("orr")), ["ssb0", "ssb1", "orr"], full("ssc"), ["ssc0", "ssc1"], gt)
-        scan("dw", "cm", "sa")
-        op("V", ["sa", "sc1"], ["xm"], lambda: V.tensor_scalar(off("xm"), ends("sa"), T.sc1[:, 0:1], 0.5, mult, gt))
         if k == 0:
             units("e1", "c1")
             own()
 
+        slot = {}
+
         def step(i, b, o):
             x, out = "z%d" % (i - 1), (el("z3", b) if i == 3 else pl("z%d" % i, b))
-            n = 2 * (i - 1) + b
-            vtt(out, ["z%d%d" % (i, b)], pl(x, b).indirect(off(o)), [x + str(b), o], pl("zd", n), ["d%d%d" % (i - 1, b)], add)
+            vtt(out, ["z%d%d" % (i, b)], pl(x, b).indirect(off(o)), [x + str(b), o], pl("zd", 2 * (i - 1) + b), ["d%d%d" % (i - 1, b)], add)
 
-        def twin(i, b):
-            n = 2 * i + b
-            op("V", ["z%d%d" % (i, b)], ["d%d%d" % (i, b)], lambda: V.tensor_copy(pl("zd", n), pl("z%d" % i, b)))
+        def far(i, b, o):
+            slot[i, b] = len(slot)
+            acopy(pl("gb", slot[i, b]), ["gb%d" % slot[i, b]], pl("z%d" % (i - 1), b).indirect(off(o)), ["z%d%d" % (i - 1, b), o])
 
-        def stream(i, b):
-            n = {1: 0, 2: 4, 3: 8}[i] + 2 * (b - 2)
-            return n * C, (n + 2) * C
+        def sums(i, b):
+            out = el("z3", b) if i == 3 else pl("z%d" % i, b)
+            one, key = (bank(4 + b), "ps%d" % (4 + b)) if i == 1 else (pl("z%d" % (i - 1), b), "z%d%d" % (i - 1, b))
+            vtt(out, ["z%d%d" % (i, b)], pl("gb", slot[i, b]), ["gb%d" % slot[i, b]], one, [key], add)
 
-        def stage(i, b, o):
-            a, e = stream(i, b)
-            s, z = stream(1, b)
-            win, one, xk = (T.st[:, s:z], T.st[:, s + 1:z:2], "u%d" % b) if i == 3 else (pl("z1", b), pl("z1", b), "z1%d" % b)
-            acopy(T.st[:, a + 1:e:2], ["y%d%d" % (i, b)], one, [xk])
-            acopy(T.st[:, a:e:2], ["w%d%d" % (i, b)], win.indirect(off(o)), [xk, o])
-
-        def pairs(i, b):
-            a, e = stream(i, b)
-            s, z = stream(1, b)
-            out, ok = (T.z3[:, b - 2:4 * C:2], ["z3%d" % b, "z3%d" % (b - 2)]) if i == 3 else (T.st[:, s:z], ["u%d" % b])
-            op("V", ["alt", "y%d%d" % (i, b), "w%d%d" % (i, b)], ok, lambda: V.tensor_tensor_scan(out, T.alt[:], T.st[:, a:e], 0.0, mult, add))
-
-        def half(b):
-            vtt(pl("z1", b), ["z1%d" % b], pl("gb", b - 2), ["gb%d" % b], bank(4 + b), ["ps%d" % (4 + b)], add)
-
-        for b in (2, 3):
-            acopy(pl("gb", b - 2), ["gb%d" % b], pl("z0", b).indirect(off(ta)), ["z0%d" % b, ta])
-        step(1, 0, ta)
-        tiny("xd", "xm", dz, mult)
-        half(2)
-        stage(2, 2, tb)
-        twin(1, 0)
+        far(1, 2, ta)
+        far(1, 3, ta)
         step(1, 1, ta)
-        half(3)
-        stage(2, 3, tb)
-        twin(1, 1)
+        far(2, 1, tb)
+        step(1, 0, ta)
+        sums(1, 2)
+        far(2, 2, tb)
+        sums(1, 3)
+        far(2, 3, tb)
+        twin(1, 0)
+        sums(2, 1)
+        far(3, 1, td)
         step(2, 0, tb)
-        pairs(2, 2)
+        sums(2, 2)
+        far(3, 2, td)
+        sums(2, 3)
+        far(3, 3, td)
+        acopy(full("sl3"), ["sl3"], full("sl2").indirect(off("o6")), ["sl2"] + o6k)
+        for b in (range(3) if k == 0 else [2]):
+            fcast(b)
         twin(2, 0)
-        op("V", [td], ["te"], lambda: V.tensor_scalar(off("te"), off(td), 2.0, 1.0, mult, add))
-        stage(3, 2, "te")
-        step(2, 1, tb)
-        pairs(2, 3)
-        stage(3, 3, "te")
-        if k == 0:
-            for b in range(3):
-                fcast(b)
-        twin(2, 1)
-        pairs(3, 2)
-        vts("xe", "xm", -2.0, 1.0, mult, add)
+        sums(3, 1)
         step(3, 0, td)
-        pairs(3, 3)
-        if k == 0:
-            quant("vt", ["vt"], "vq", "vqs", 128)
-        for h, (a, e) in enumerate(halves):
-            vtt(T.z3[:, 4 * a + 1:4 * e:4], ["z31" + "ab"[h]], pl("z2", 1).indirect(off(td, h)), ["z21", "z31", td], T.zd[:, 5 * C + a:5 * C + e], ["d21"], add)
+        sums(3, 2)
+        sums(3, 3)
         zk = parts(zq)
         for h in (0, 1):
-            quant_half("z3", ["z30", "z31", "z32", "z33"] + parts("z31")[0:h + 1], zq, zs, h)
+            quant_half("z3", ["z30", "z31", "z32", "z33"], zq, zs, h)
             mm(h, "wq", 0, ["wqc", "wqp"], zq, zs, [zk[h]], *halves[h])
 
-        tiny(lz1, lz, "xd", add)
-        tiny(dz1, dz, "xe", mult)
-        if last:
-            op("V", [lz1], ["loa"], lambda: V.tensor_copy(T.lo[:, 0:K], off(lz1)))
-            tiny("l1f", lz1, dz1, add)
-            op("V", ["l1f"], ["lob"], lambda: V.tensor_copy(T.lo[:, K:2 * K], off("l1f")))
+        vtt(full("cm"), ["cm"], full("sl3").indirect(off("o6")), ["sl3"] + o6k, full("ssb"), ["ssb0", "ssb1"], gt)
 
         for b in (1, 3, 2):
             mm(4 + b, "wq", 128 * b, ["wqc", "wqp"], zq, zs, zk)
-        op("V", ["ps0"], ["hb0a"], lambda: V.tensor_scalar(T.hb[:, 0:CUT], bank(0, CUT), 0.03125, None, mult))
+        acopy(T.hb[:, 0:CUT], ["hb0a"], bank(0, CUT), ["ps0"], 0.03125)
         acopy(T.hb[:, CUT:C], ["hb0b"], bank(1, C - CUT), ["ps1"], 0.03125)
+        vscan(full("sa"), ["sa"], full("dw"), full("cm"), ["dw", "cm"])
         for b in (1, 3, 2):
             acopy(pl("hb", b), ["hb%d" % b], bank(4 + b), ["ps%d" % (4 + b)], 0.03125)
         acopy(full("xg"), ["xg"], pl("hb", 3).indirect(off(pt)), ["hb3", pt])
+        op("A", ["sa", "thr"], ["xe"], lambda: A.activation(off("xe"), ends("sa"), sign, bias=T.thr[:, 0:1], scale=-1.0))
+        if k == 0:
+            quant("vt", ["vt"], "vq", "vqs", 128)
         for b in range(3):
             vtt(el(nx, b), [nx + "_%d" % b], pl("hb", b).indirect(off(pt)), ([] if b else ["hb0a", "hb0b"]) + ["hb%d" % b, pt], pl("fo", b), ["fo%d" % b], add)
         for h, (a, e) in enumerate(halves):
-            vtt(T[nx][:, 4 * a + 3:4 * e:4], [nx + "_%d" % (3 + h)], T.xg[:, a:e], ["xg"], T.ps3[:, a:e], ["ps3"], add)
-        if last:
-            acopy(T.lrep[:], ["lrep"], full("fi").indirect(T.lo[:, 0:2 * K]), ["fi", "loa", "lob"])
-            dma("Y", "dls", ["lrep"], [], T.ls[:], T.lrep[0:128:16, :])
+            vtt(el(nx, 3, h), [nx + "_%d" % (3 + h)], T.xg[:, a:e], ["xg"], T.ps3[:, a:e], ["ps3"], add)
+        vtt(dz, ["dz"], dz, ["dz"], off("xe"), ["xe"], mult)
 
     xq, xs = "xq%d" % ROUNDS, "xs%d" % ROUNDS
     xk = parts(xq)
+    vts(off("hd"), ["hd"], dz, ["dz"], 0.5, None, mult)
     for h in (0, 1):
         quant_half("xt%d" % ROUNDS, ["xt%d_%d" % (ROUNDS, b) for b in range(4 + h)], xq, xs, h)
         mm(h, "vq", 0, ["vq"], xq, xs, [xk[h]], *halves[h])
+        vtt(off("l%df" % h), ["l%df" % h], mid, ["mid"], off("hd"), ["hd"], add if h else sub)
+    for h in (0, 1):
+        vcopy(T.lo[:, h * K:h * K + K], ["lo%d" % h], off("l%df" % h), ["l%df" % h])
     dma("Y", "doc", xk, [], T.oc[:], full(xq).bitcast(dt.uint8))
     for i in range(4):
         dma("Y", "dsc%d" % i, xk, [], T.osc[4 * i:4 * i + 4, :], T[xs][32 * i:32 * i + 4, :])
     acopy(T.yo[:, 0:CUT], ["yo0"], bank(0, CUT), ["ps0"])
-    op("V", ["ps1"], ["yo1"], lambda: V.tensor_copy(T.yo[:, CUT:C], bank(1, C - CUT)))
+    vcopy(T.yo[:, CUT:C], ["yo1"], bank(1, C - CUT), ["ps1"])
     dma("A", "dy0", ["yo0"], [], T.y[:, 0:CUT], T.yo[:, 0:CUT])
     dma("Y", "dy1", ["yo1"], [], T.y[:, CUT:C], T.yo[:, CUT:C])
+    acopy(T.lrep[:, 0:C], ["lrep0"], full("fi").indirect(T.lo[:, 0:K]), ["fi", "lo0"])
+    vcopy(T.lrep[:, C:2 * C], ["lrep1"], full("fi").indirect(T.lo[:, K:2 * K]), ["fi", "lo1"])
+    dma("A", "dls", ["lrep0", "lrep1"], [], T.ls[:], T.lrep[0:128:16, :])
     for s in total:
         if known["Y"].get(s, 0) < total[s]:
             Q["Y"].wait_ge(T.sem[s], total[s])

@@ -6,9 +6,15 @@ STEP = [4, 1, 2]
 ROUNDS = len(STEP)
 HALF = C // 2
 CUT = 160
-WHOLE = 1024.0
+LIFT = 512.0
 
-ORDER = "Lw Da Db sa sb ta pa tb pb ma mb"
+SCORES = "ba bb ga gb ea eb wa wb dw sa sb pw keep"
+FIRST = "Kw sb sa La tb pb ta pa Lb da db ma mb"
+ORDER = "Da Db sa xw sb ta pa tb pb ma mb xw"
+LAST = "Da Db sa xw sb ta tb ma mb"
+MIDDLE = "l8 c0 c1 c2 c3 F0 F1 hold ea ne o8 eb S1 mini wa wb p2 pt q1a q1b t00 S2 huw tuw Gu q2b t01 q2a hvw tvw Gv f12 f13 s11 f21 a12 s10 a13 t10 a21 f22 s20 f23 a22 a23 f31 f32 t20 a31 s30 f33 S3 a32 a33a a33b F2"
+STATE = "qa qb cm m1 m3 m2 h0a h0b hc h1 xe h3 h2 xg xt n0 dz n1 hd n2 n3a n3b"
+LATER = "dz hd"
 
 SCRATCH = {}
 
@@ -26,22 +32,22 @@ def _declare():
             s[n + str(k)] = ("sbuf", [128, 32], "uint16")
         s["zq%d" % k] = ("sbuf", [128, C], "float8_e4m3fn_x4")
         s["zs%d" % k] = ("sbuf", [128, C], "uint8")
-    for n, w in (("ut", 512), ("vt", 512), ("em", 520), ("en", 2 * C), ("e1", 520), ("e8", 520), ("ic", C), ("mk", C),
-                 ("dw", C), ("sa", C), ("sb", C), ("sc", C), ("sd", C), ("cm", C), ("l2s", C),
-                 ("q0", C), ("q1", C), ("q2", C), ("xg", C), ("tab", 24 * C), ("zd", 6 * C),
-                 ("fo", 4 * C), ("z0", 4 * C), ("z1", 4 * C), ("z2", 4 * C), ("z3", 4 * C), ("gb", 8 * C), ("hb", 4 * C)):
+    for n, w in (("ut", 512), ("vt", 512), ("en", 520), ("e1", 520), ("ic", C), ("mk", C), ("jj", C), ("m1", C), ("wa", C),
+                 ("dw", C), ("cm", C), ("l2s", C), ("xw", C), ("pp", 2 * C), ("tq", 2 * C), ("lt", 2 * C),
+                 ("q0", C), ("q1", C), ("q2", C), ("xg", C), ("tab", 24 * C), ("zd", 12 * C),
+                 ("fo", 4 * C), ("z0", 4 * C), ("z1", 4 * C), ("z2", 4 * C), ("z3", 4 * C), ("gb", 12 * C), ("hb", 4 * C)):
         s[n] = ("sbuf", [128, w], "bfloat16")
-    for n, w in (("sg", 2 * C), ("sw", 2 * C), ("sp", 2 * C), ("tz", 64), ("tp", 64), ("to", 64), ("le", 24)):
+    for n, w in (("sg", 2 * C), ("sw", 2 * C), ("sp", 2 * C), ("tg", 2 * C), ("tw", 2 * C), ("dd", 2 * C), ("tz", 64), ("tp", 64), ("to", 64),
+                 ("sa", C), ("sb", C), ("sc", C), ("sd", C), ("se", C), ("sf", C), ("lm", C)):
         s[n] = ("sbuf", [128, w], "float16")
-    for n, w in (("ol", 32 * 9), ("snt", 32 * 3 * ROUNDS), ("uo", 32)):
+    for n, w in (("ol", 32 * 10), ("snt", 32 * 3 * ROUNDS), ("uo", 32), ("lo", 64), ("li", 64)):
         s[n] = ("sbuf", [128, w], "uint16")
-    s["lo"] = ("sbuf", [128, 64], "uint16")
-    for n, w in (("ri", C), ("rr", C), ("pi", 8), ("pj", 8), ("k16", 24), ("uj", 8), ("la32", 24), ("lb32", 24)):
+    for n, w in (("pi", 8), ("pj", 8), ("k16", 24), ("uj", 8), ("la32", 24), ("lb32", 24)):
         s[n] = ("sbuf", [128, w], "int32")
-    for n, w in (("wa", C), ("m1", C), ("ssb", C), ("sl1", C), ("sl2", C), ("sl3", C), ("fi", C), ("lrep", 2 * C), ("yo", C), ("sc0", 8), ("sc1", 8), ("thr", 8),
-                 ("pf", 8), ("cw", 24), ("cv", 24), ("xe", 24), ("sm", 24), ("hd", 24), ("l0f", 24), ("l1f", 24)):
+    for n, w in (("ssb", C), ("sl1", C), ("sl2", C), ("sl3", C), ("fi", C), ("lrep", 2 * C), ("yo", C), ("sc0", 8), ("sc1", 8), ("thr", 8),
+                 ("pf", 8), ("pn", 8), ("cw", 24), ("cv", 24), ("xe", 24), ("sm", 24), ("hd", 24), ("lf", 48)):
         s[n] = ("sbuf", [128, w], "float32")
-    for n, w in (("uq", 128), ("uq2", 128), ("vq", 128), ("wq", 512), ("c1", 512), ("c8", 512)):
+    for n, w in (("uq", 128), ("uq2", 128), ("vq", 128), ("wq", 512), ("c1", 512)):
         s[n] = ("sbuf", [128, w], "float8_e4m3fn_x4")
         s[n + "s"] = ("sbuf", [128, w], "uint8")
     for i in range(8):
@@ -49,7 +55,7 @@ def _declare():
 
 
 _declare()
-SEMAPHORES = (["eV", "eA", "eP", "eG", "lsem"] + ["dx", "du", "dla", "dlb", "dwc", "dws", "dv", "dls", "doc", "dy0", "dy1"] + ["dsc%d" % i for i in range(4)]
+SEMAPHORES = (["eV", "eA", "eP", "eG", "left", "left0", "left1"] + ["dx", "du", "dla", "dlb", "dwc", "dws", "dv", "dls", "doc", "dy0", "dy1"] + ["dsc%d" % i for i in range(4)]
               + ["%s%d" % (n, k) for n in ("rx", "ra", "rb", "rd") for k in range(ROUNDS)])
 
 
@@ -109,8 +115,9 @@ def rank_program(g, core, T, topo):
     def send(dst, sem, reads, out, in_):
         before("G", reads, [])
         rid, pid = topo.addr(dst, core)
-        g.remote_dma(out, in_, T.sem[sem], T.sem.lsem, pid, rid, topo.mask(core, dst))
-        total["lsem"] = total.get("lsem", 0) + len(topo.engines(core, dst))
+        left = {"rx0": "left0", "rx1": "left1"}.get(sem, "left")
+        g.remote_dma(out, in_, T.sem[sem], T.sem[left], pid, rid, topo.mask(core, dst))
+        total[left] = total.get(left, 0) + len(topo.engines(core, dst))
 
     def lands(src, sem, buf, writes=1):
         n = writes * len(topo.engines(src, core))
@@ -122,15 +129,18 @@ def rank_program(g, core, T, topo):
     V, A, P = g.vector, g.scalar, g.tensor
     mult, add, sub, lt, gt, eq, ne, amin = (AluOpType.mult, AluOpType.add, AluOpType.subtract, AluOpType.is_lt, AluOpType.is_gt, AluOpType.is_equal,
                                             AluOpType.not_equal, AluOpType.min)
-    copy, sign = ActivationFunctionType.Copy, ActivationFunctionType.Sign
+    copy, sign, same = ActivationFunctionType.Copy, ActivationFunctionType.Sign, ActivationFunctionType.Identity
     tables = {n: i * C for i, n in enumerate(["t%d" % i for i in range(9)] + ["l%d" % i for i in range(9)] + ["k%d" % i for i in range(1, 7)])}
 
     halves = ((0, CUT), (CUT, C))
     wide = (CUT, C - CUT)
     runs = ((0, CUT // 16), (CUT // 16, K))
 
-    def parts(n):
-        return [n + "a", n + "b"]
+    def parts(n, h=None):
+        return [n + "a", n + "b"] if h is None else [n + "ab"[h]]
+
+    def half(c):
+        return None if c == "w" else "ab".index(c)
 
     def full(n, h=None):
         a, e = (0, C) if h is None else halves[h]
@@ -138,7 +148,11 @@ def rank_program(g, core, T, topo):
             return T.tab[:, tables[n] + a:tables[n] + e]
         return T[n][:, a:e]
 
-    picks = {n: i * 32 for i, n in enumerate(["o%d" % i for i in range(9)])}
+    def pairs(n, h=None, first=0, step=1):
+        a, e = (0, C) if h is None else halves[h]
+        return T[n][:, 2 * a + first:2 * e:step]
+
+    picks = {n: i * 32 for i, n in enumerate(["o%d" % i for i in range(10)])}
     sent = {n + str(i): (3 * i + j) * 32 for i in range(ROUNDS) for j, n in enumerate(["pt", "pu", "pv"])}
 
     def off(n, h=None):
@@ -179,20 +193,21 @@ def rank_program(g, core, T, topo):
     def acopy(out, ok, in_, ik, scale=1.0):
         op("A", ik, ok, lambda: A.activation(out, in_, copy, scale=scale))
 
-    def wrap(src, sk, sn, out, ok):
-        vscan(full(sn), [sn], full("dw"), full(src), ["dw"] + sk)
-        vts(off(out), ok, ends(sn), [sn, "sc1"], T.sc1[:, 0:1], 144.25, mult, add)
+    def hold(sn, ok, src, sk, h=None):
+        op("V", ["dw"] + sk, ok, lambda: V.tensor_tensor_scan(full(sn, h), full("dw", h), full(src, h), 0.0, add, AluOpType.max))
 
-    def shared(win, wk, o, ok, out):
-        acopy(full(out, 0), [parts(out)[0]], full(win).indirect(off(o, 0)), wk + ok)
-        vcopy(full(out, 1), [parts(out)[1]], full(win).indirect(off(o, 1)), wk + ok)
+    def offsets(out, ok, sn, sk, h=None):
+        vts(off(out, h), ok, ends(sn, h), sk + ["sc1"], T.sc1[:, 0:1], None, add)
+
+    def gather(h, win, wk, o, ok, out):
+        (vcopy if h else acopy)(full(out, h), parts(out, h), win.indirect(off(o, h)), wk + ok)
 
     def quant(t, tk, q, s, w=C):
         op("V", tk, [q], lambda: V.quantize_mx(T[q][:, 0:w], T[s][:, 0:w], T[t][:, 0:4 * w]))
 
     def quant_half(t, tk, q, s, h):
         a, e = halves[h]
-        op("V", tk, [parts(q)[h]], lambda: V.quantize_mx(T[q][:, a:e], T[s][:, a:e], T[t][:, 4 * a:4 * e]))
+        op("V", tk, parts(q, h), lambda: V.quantize_mx(T[q][:, a:e], T[s][:, a:e], T[t][:, 4 * a:4 * e]))
 
     def units(e, c, which=range(4)):
         for b in which:
@@ -206,52 +221,45 @@ def rank_program(g, core, T, topo):
     def iota(out, ok, pattern, base, cm):
         op("G", [], [ok], lambda: g.iota(out, pattern, base, cm, allow_small_or_imprecise_dtypes=True))
 
-    def fill(out, ok, x):
-        op("V", [], ok, lambda: V.memset(out, x))
-
     dma("Y", "dx", [], ["xt0"], T.xt0[:], T.x[:])
     dma("A", "du", [], ["ut"], T.ut[:], T.u[:])
     dma("Y", "dla", [], ["la32"], off("la32"), T.la[:])
     dma("A", "dlb", [], ["lb32"], off("lb32"), T.lb[:])
-    fill(T.em[:], ["em"], 0.125)
-    fill(T.en[:], ["en"], 1.0)
-    iota(T.ri[:], "ri", [[-1, C]], C, 1)
+    op("V", [], ["en"], lambda: V.memset(T.en[:], 1.0))
     iota(T.pi[:, 0:1], "pi", [[0, 1]], 0, 1)
     iota(T.uj[:, 0:8], "uj", [[16, 8]], 0, 0)
     iota(off("k16"), "k16", [[16, K]], 0, 0)
+    iota(T.jj[:], "jj", [[0, K], [1, 16]], 0, 0)
+    op("G", ["en"], ["e1"], lambda: g.affine_select(T.e1[:], T.en[:], [[1, 520]], eq, 0.0, -4, -4))
     iota(T.ic[:], "ic", [[1, C]], -HALF, 0)
-    op("G", ["em"], ["e8"], lambda: g.affine_select(T.e8[:], T.em[:], [[1, 520]], eq, 0.0, -4, -4))
 
-    s1 = T.sc1[:, 0:1]
-    vts(full("rr"), ["rr"], full("ri"), ["ri"], 15, None, AluOpType.bitwise_and)
+    s1, pf, pn = T.sc1[:, 0:1], T.pf[:, 0:1], T.pn[:, 0:1]
+    dz, mid = T.sw[:, 31:2 * C:32], T.sg[:, 31:2 * C:32]
     vts(T.pj[:, 0:1], ["pj"], T.pi[:, 0:1], ["pi"], 15, None, AluOpType.bitwise_and)
     vcopy(T.uo[:, 0:8], ["uo"], T.uj[:, 0:8], ["uj"])
-    vts(full("m1"), ["m1"], full("rr"), ["rr"], 1.0, None, amin)
-    vts(full("wa"), ["wa"], full("rr"), ["rr"], 15.0, 65535.0, eq, mult)
-    vts(T.sc0[:, 0:1], ["sc0"], T.pj[:, 0:1], ["pj"], 15.0, 1.0 - 2.0 ** -16, eq, mult)
-    vcopy(T.pf[:, 0:1], ["pf"], T.pj[:, 0:1], ["pj"])
-    vts(full("mk"), ["mk"], full("m1"), ["m1"], -1e29, None, mult)
-    vcopy(T.sw[:], ["sw", "dz"], T.en[:], ["en"])
-    vts(T.sg[:], ["sg", "sg0", "sg1", "mid"], T.en[:], ["en"], 0.0, None, mult)
-    vtt(full("dw"), ["dw"], full("wa"), ["wa"], full("m1"), ["m1"], add)
-    vts(s1, ["sc1"], T.sc0[:, 0:1], ["sc0"], 2.0 ** -16, None, add)
-    vts(off("cw"), ["cw"], off("k16"), ["k16", "pf"], T.pf[:, 0:1], None, add)
-    vts(T.sw[:, 0:2 * C:32], ["sw"], off("k16"), ["k16"], 0.0, None, mult)
-    vts(T.sg[:, 1:2 * C:32], ["sg"], off("k16"), ["k16"], 0.0, -0.5, mult, add)
-    dz, mid, chosen = T.sw[:, 31:2 * C:32], T.sg[:, 31:2 * C:32], T.sp[:, 31:2 * C:32]
+    vts(T.tz[:, 0:3 * K:3], ["tz0"], off("k16"), ["k16"], 0.0, None, mult)
+    vcopy(pf, ["pf"], T.pj[:, 0:1], ["pj"])
+    vts(pn, ["pn"], T.pj[:, 0:1], ["pj"], 1.0, None, add)
+    vts(T.sc0[:, 0:1], ["sc0"], T.pj[:, 0:1], ["pj"], 15.0, LIFT, ne, mult)
+    vts(T.tz[:, 1:3 * K:3], ["tz1"], off("k16"), ["k16"], 0.0, 1.0, mult, add)
+    vts(off("cw"), ["cw"], off("k16"), ["k16", "pf"], pf, None, add)
+    vts(s1, ["sc1"], T.sc0[:, 0:1], ["sc0"], -1.0, float(HALF), mult, add)
+    vts(T.thr[:, 0:1], ["thr"], T.sc0[:, 0:1], ["sc0"], 0.5, None, add)
+    vts(T.tp[:, 1:3 * K:3], ["tp1"], off("cw"), ["cw"], -1.0, None, mult)
+    vcopy(T.tp[:, 2:3 * K:3], ["tp2"], off("cw"), ["cw"])
+    vts(off("cv"), ["cv"], off("cw"), ["cw", "sc1"], s1, None, sub)
+    vts(pairs("sw", None, 1, 2), ["dz"], full("jj"), ["jj"], 0.0, 1.0, mult, add)
+    vts(pairs("sg", None, 1, 2), ["mid"], full("jj"), ["jj"], 0.0, -0.5, eq, mult)
+    vts(pairs("sw", None, 0, 2), ["sw"], full("jj"), ["jj"], 0.0, None, ne)
+    vts(full("mk"), ["mk"], full("jj"), ["jj", "pf"], pf, -1e29, ne, mult)
+    vts(full("m1"), ["m1"], full("jj"), ["jj", "pf"], pf, -16384.0, eq, mult)
+    vts(full("wa"), ["wa"], full("jj"), ["jj", "pn"], pn, LIFT, eq, mult)
     quant("ut", ["ut"], "uq", "uqs", 128)
+    vtt(full("dw"), ["dw"], full("wa"), ["wa"], full("m1"), ["m1"], add)
     vcopy(T.uq2[:, 0:128].bitcast(dt.uint32), ["uq2c"], T.uq[:, 0:128].bitcast(dt.uint32).indirect(T.uo[:, 0:8]), ["uq", "uo"])
     op("A", ["uq", "uo"], ["uq2p"], lambda: A.activation(T.uq2s[:, 0:128], T.uqs[:, 0:128].indirect(T.uo[:, 0:8]), copy))
 
-    def late_constants():
-        vts(T.thr[:, 0:1], ["thr"], T.pj[:, 0:1], ["pj"], 15.0, 0.5 - 2.0 ** 15, eq, mult)
-        vts(T.tz[:, 0:3 * K:3], ["tz0"], off("k16"), ["k16"], 0.0, None, mult)
-        vts(T.tz[:, 1:3 * K:3], ["tz1"], off("k16"), ["k16"], 0.0, 1.0, mult, add)
-        vts(T.thr[:, 0:1], ["thr"], T.thr[:, 0:1], ["thr"], 2.0 ** 15, None, add)
-        vts(T.tp[:, 1:3 * K:3], ["tp1"], off("cw"), ["cw"], -1.0, None, mult)
-        vcopy(T.tp[:, 2:3 * K:3], ["tp2"], off("cw"), ["cw"])
-        vts(off("cv"), ["cv"], off("cw"), ["cw"], WHOLE, None, add)
-
+    later = []
     for k in range(ROUNDS):
         dst, src = T.cores[(rank + STEP[k]) % 8], T.cores[(rank - STEP[k]) % 8]
         xt, xq, xs, aq, asc, zq, zs = [n + str(k) for n in ("xt", "xq", "xs", "aq", "as", "zq", "zs")]
@@ -269,193 +277,232 @@ def rank_program(g, core, T, topo):
             for b in range(4):
                 mm(b, "c1", 128 * b, ["c1%d" % b], xq, xs, xk)
 
-        def fcast(b):
-            acopy(pl("fo", b), ["fo%d" % b], bank(b), ["ps%d" % b])
-
         for h in (0, 1):
             quant_half(xt, [xt] + [xt + "_%d" % b for b in range(4 + h)], xq, xs, h)
-            mm(4 + h, "uq2", 0, ["uq2c", "uq2p"], xq, xs, [xk[h]], *halves[h])
+            for i in (4 + h, 6 + h):
+                mm(i, "uq2", 0, ["uq2c", "uq2p"], xq, xs, [xk[h]], *halves[h])
+        for c in LATER.split() if k else []:
+            later[0](c)
         send(dst, "rx%d" % k, xk, full(aq).bitcast(dt.uint8), full(xq).bitcast(dt.uint8))
         send(dst, "rx%d" % k, xk, full(asc), full(xs))
         if k:
             own()
         else:
-            op("G", ["en"], ["e1"], lambda: g.affine_select(T.e1[:], T.en[:, 0:520], [[1, 520]], eq, 0.0, -4, -4))
             iota(T.fi[:], "fi", [[1, C]], 0, 0)
-            wait_for("Y", [("dx", 16)])
-            dma("Y", "dwc", [], ["wqc"], T.wq[:].bitcast(dt.uint8), T.wc[:])
-            dma("Y", "dws", [], ["wqp"], T.wqs[:], T.ws[:])
-            dma("Y", "dv", [], ["vt"], T.vt[:], T.v[:])
             vtt(off("sm"), ["sm"], off("la32"), ["la32"], off("lb32"), ["lb32"], add)
             vtt(dz, ["dz"], off("lb32"), ["lb32"], off("la32"), ["la32"], sub)
+            vcopy(T.li[:, 0:K], ["lia"], off("la32"), ["la32"])
+            vcopy(T.li[:, K:2 * K], ["lib"], off("lb32"), ["lb32"])
             vts(mid, ["mid"], off("sm"), ["sm"], 0.5, None, mult)
+        if k < 2:
+            wait_for("Y", [("left%d" % k, total["left%d" % k])])
+            if k:
+                dma("Y", "dv", [], ["vt"], T.vt[:], T.v[:])
+            else:
+                dma("Y", "dwc", [], ["wqc"], T.wq[:].bitcast(dt.uint8), T.wc[:])
+                dma("Y", "dws", [], ["wqp"], T.wqs[:], T.ws[:])
 
-        for h, (a, e) in enumerate(halves):
-            vtt(T.sg[:, 2 * a:2 * e:2], ["sg%d" % h], bank(4 + h, wide[h]), ["ps%d" % (4 + h)], full("mk", h), ["mk"], lt)
-        for h, (a, e) in enumerate(halves):
-            vscan(T.sp[:, 2 * a:2 * e], [parts("sp")[h]], T.sw[:, 2 * a:2 * e], T.sg[:, 2 * a:2 * e], ["sw", "dz", "sg", "sg%d" % h, "mid"])
-        for h, (a, e) in enumerate(halves):
-            vcopy(off("o0", h), [parts("o0")[h]], T.sp[:, 2 * a + 31:2 * e:32], [parts("sp")[h]])
-        for h in (0, 1):
-            acopy(full("ssb", h), ["ssb%d" % h], bank(4 + h, wide[h]), ["ps%d" % (4 + h)])
-
-        acopy(full("t0", 0), ["t0a"], full("ic").indirect(off("o0", 0)), ["ic", "o0a"])
-        vcopy(T.tp[:, 0:3 * K:3], ["tp0"], chosen, parts("sp"))
-        vcopy(full("t0", 1), ["t0b"], full("ic").indirect(off("o0", 1)), ["ic", "o0b"])
-        shared("t0", parts("t0"), "o0", parts("o0"), "t1")
-        shared("t1", parts("t1"), "o0", parts("o0"), "t2")
-        vtt(full("l2s"), ["l2s"], full("t0"), parts("t0"), full("t1"), parts("t1"), amin)
-        def level(c, j):
-            h = "ab".index(c[1]) if c[1] != "w" else None
-            sn, o, t, nt, l, m, kj = "sc" if j % 2 else "sd", "o%d" % j, "t%d" % (j + 1), "t%d" % (j + 2), "l%d" % j, "l%d" % (j + 1), "k%d" % j
-
-            def key(n):
-                return parts(n) if h is None else [parts(n)[h]]
-
-            if j < 1 or j > 6:
-                return
+        def scores(c):
+            h = half(c[1]) if len(c) == 2 else None
+            if c[0] == "b":
+                vtt(pairs("sg", h, 0, 2), parts("sg", h), bank(4 + h, wide[h]), ["ps%d" % (4 + h)], full("mk", h), ["mk"], lt)
+            if c[0] == "e":
+                vscan(pairs("sp", h), parts("sp", h), pairs("sw", h), pairs("sg", h), ["sw", "dz", "mid"] + parts("sg", h))
+            if c[0] == "p":
+                vcopy(off("o0", h), parts("o0", h), pairs("sp", h, 31, 32), parts("sp", h))
             if c[0] == "s":
-                vscan(full(sn, h), key(sn), full("dw", h), full(t, h), ["dw"] + key(t))
-            if c[0] == "t":
-                vts(off(o, h), key(o), ends(sn, h), key(sn) + ["sc1"], s1, 144.25, mult, add)
-            if c[0] == "p" and j < 6:
-                acopy(full(nt, h), key(nt), full(t).indirect(off(o, h)), parts(t) + key(o))
-            if c[0] == "m":
-                vtt(full(m, h), key(m), full(l).indirect(off(o, h)), parts(l) + key(o), full(kj, h), key(kj), amin)
+                acopy(full("ssb", h), parts("ssb", h), bank(6 + h, wide[h]), ["ps%d" % (6 + h)])
+            if c == "keep":
+                vcopy(T.tp[:, 0:3 * K:3], ["tp0"], pairs("sp", None, 31, 32), parts("sp"))
+            if k and c[0] == "g":
+                op("A", ["ps%d" % (6 + h)], parts("tg", h), lambda: A.activation(pairs("tg", h, 0, 2), bank(6 + h, wide[h]), sign, bias=2.0 ** -93))
+            if k and c[0] == "w":
+                vscan(pairs("pp", h), parts("pp", h) + parts("fl", h), pairs("tw", h), pairs("tg", h), ["tw0"] + parts("tw1", h) + parts("tg1", h) + parts("tg", h))
             if c[0] == "d":
-                vcopy(full(kj, h), key(kj), full(l, h), key(l))
-            if c[0] == "D":
-                acopy(full(kj, h), key(kj), full(l, h), key(l))
-            if c[0] == "L" and j == 1:
-                vtt(full(l), parts(l), full("l2s"), ["l2s"], full("t2"), parts("t2"), amin)
+                vts(off("o7", h), parts("o7", h), pairs("sp", h, 31, 32), parts("sp", h), 2.0, 1.0, mult, add)
 
-        for j in range(1, 8):
-            for c in ORDER.split():
-                level(c, j - (int(c[2]) if len(c) > 2 else 0))
-            if k == 0 and j < 5:
-                units("e8", "c8", [j - 1])
-            if k == 0 and j == 5:
-                late_constants()
-        o6k = parts("o6")
-        vtt(full("l8"), ["l8"], full("l7").indirect(off("o6")), parts("l7") + o6k, full("l6"), parts("l6"), amin)
+        for c in SCORES.split():
+            if k == 0 and c == "sb":
+                acopy(T.lt[:], ["lt"], full("ic").indirect(T.li[:, 0:2 * K]), ["ic", "lia", "lib"], 0.5)
+            else:
+                scores(c)
 
-        for b in range(4):
-            mm(4 + b, "c8", 128 * b, ["c8%d" % b], aq, asc, [aq])
-        for b in range(4):
-            acopy(pl("z0", b), ["z0%d" % b], bank(4 + b), ["ps%d" % (4 + b)])
-        if k:
-            for b in range(2):
-                fcast(b)
-
-        vscan(full("sa"), ["sa"], full("dw"), full("l8"), ["dw", "l8"])
-        vts(off("le"), ["le"], ends("sa"), ["sa", "sc1"], s1, WHOLE + HALF, mult, add)
-        vts(off("o8"), ["o8"], ends("sa"), ["sa", "sc1"], s1, 144.25, mult, add)
-        vtt(T.tz[:, 2:3 * K:3], ["tz2"], off("le"), ["le"], off("cv"), ["cv"], ne)
-        vscan(T.to[:, 0:3 * K], ["to"], T.tz[:, 0:3 * K], T.tp[:, 0:3 * K], ["tz0", "tz1", "tz2", "tp0", "tp1", "tp2"])
-        vcopy(off(pt), [pt], T.to[:, 2:3 * K:3], ["to"])
-        send(dst, "ra%d" % k, [pt], off(ta), off(pt))
-
-        def twin(i, b):
-            vcopy(pl("zd", 2 * i + b), ["d%d%d" % (i, b)], pl("z%d" % i, b), ["z%d%d" % (i, b)])
-
-        twin(0, 1)
-        shared("ic", ["ic"], pt, [pt], "q0")
-        shared("q0", parts("q0"), pt, [pt], "q1")
-        acopy(full("sl1"), ["sl1"], full("ssb").indirect(off("o8")), ["ssb0", "ssb1", "o8"])
-        wrap("q1", parts("q1"), "sb", pu, [pu])
-        send(dst, "rb%d" % k, [pu], off(tb), off(pu))
-        twin(0, 0)
-        shared("q1", parts("q1"), pu, [pu], "q2")
-        acopy(full("sl2"), ["sl2"], full("sl1").indirect(off("o6")), ["sl1"] + o6k)
-        wrap("q2", parts("q2"), "sa", pv, [pv])
-        send(dst, "rd%d" % k, [pv], off(td), off(pv))
         if k == 0:
-            units("e1", "c1")
-            own()
-
-        slot = {}
-
-        def step(i, b, o):
-            x, out = "z%d" % (i - 1), (el("z3", b) if i == 3 else pl("z%d" % i, b))
-            vtt(out, ["z%d%d" % (i, b)], pl(x, b).indirect(off(o)), [x + str(b), o], pl("zd", 2 * (i - 1) + b), ["d%d%d" % (i - 1, b)], add)
-
-        def far(i, b, o):
-            slot[i, b] = len(slot)
-            acopy(pl("gb", slot[i, b]), ["gb%d" % slot[i, b]], pl("z%d" % (i - 1), b).indirect(off(o)), ["z%d%d" % (i - 1, b), o])
-
-        def sums(i, b):
-            out = el("z3", b) if i == 3 else pl("z%d" % i, b)
-            one, key = (bank(4 + b), "ps%d" % (4 + b)) if i == 1 else (pl("z%d" % (i - 1), b), "z%d%d" % (i - 1, b))
-            vtt(out, ["z%d%d" % (i, b)], pl("gb", slot[i, b]), ["gb%d" % slot[i, b]], one, [key], add)
-
-        far(1, 2, ta)
-        far(1, 3, ta)
-        step(1, 1, ta)
-        far(2, 1, tb)
-        step(1, 0, ta)
-        sums(1, 2)
-        far(2, 2, tb)
-        sums(1, 3)
-        far(2, 3, tb)
-        twin(1, 0)
-        sums(2, 1)
-        far(3, 1, td)
-        step(2, 0, tb)
-        sums(2, 2)
-        far(3, 2, td)
-        sums(2, 3)
-        far(3, 3, td)
-        acopy(full("sl3"), ["sl3"], full("sl2").indirect(off("o6")), ["sl2"] + o6k)
-        for b in (range(3) if k == 0 else [2]):
-            fcast(b)
-        twin(2, 0)
-        sums(3, 1)
-        step(3, 0, td)
-        sums(3, 2)
-        sums(3, 3)
-        zk = parts(zq)
+            for h in (0, 1):
+                (vcopy if h else acopy)(pairs("pp", h, 1, 2), parts("pp", h), full("ic").indirect(off("o0", h)), ["ic"] + parts("o0", h))
+            scores("sb")
+            vts(pairs("pp", None, 0, 2), ["pe"], full("jj"), ["jj"], 0.0, None, mult)
+            units("e1", "c1", [0])
         for h in (0, 1):
-            quant_half("z3", ["z30", "z31", "z32", "z33"], zq, zs, h)
-            mm(h, "wq", 0, ["wqc", "wqp"], zq, zs, [zk[h]], *halves[h])
-
-        vtt(full("cm"), ["cm"], full("sl3").indirect(off("o6")), ["sl3"] + o6k, full("ssb"), ["ssb0", "ssb1"], gt)
-
-        for b in (1, 3, 2):
-            mm(4 + b, "wq", 128 * b, ["wqc", "wqp"], zq, zs, zk)
-        acopy(T.hb[:, 0:CUT], ["hb0a"], bank(0, CUT), ["ps0"], 0.03125)
-        acopy(T.hb[:, CUT:C], ["hb0b"], bank(1, C - CUT), ["ps1"], 0.03125)
-        vscan(full("sa"), ["sa"], full("dw"), full("cm"), ["dw", "cm"])
-        for b in (1, 3, 2):
-            acopy(pl("hb", b), ["hb%d" % b], bank(4 + b), ["ps%d" % (4 + b)], 0.03125)
-        acopy(full("xg"), ["xg"], pl("hb", 3).indirect(off(pt)), ["hb3", pt])
-        op("A", ["sa", "thr"], ["xe"], lambda: A.activation(off("xe"), ends("sa"), sign, bias=T.thr[:, 0:1], scale=-1.0))
+            gather(h, T.pp[:], parts("pp") + ["pe"], "o7", parts("o7", h), "t1")
+        vtt(pairs("dd", None, 1, 2), parts("dd"), full("ic"), ["ic"], pairs("pp", None, 1, 2), parts("pp"), sub)
+        spare = [lambda: quant("vt", ["vt"], "vq", "vqs", 128)] if last else []
         if k == 0:
-            quant("vt", ["vt"], "vq", "vqs", 128)
-        for b in range(3):
-            vtt(el(nx, b), [nx + "_%d" % b], pl("hb", b).indirect(off(pt)), ([] if b else ["hb0a", "hb0b"]) + ["hb%d" % b, pt], pl("fo", b), ["fo%d" % b], add)
-        for h, (a, e) in enumerate(halves):
-            vtt(el(nx, 3, h), [nx + "_%d" % (3 + h)], T.xg[:, a:e], ["xg"], T.ps3[:, a:e], ["ps3"], add)
-        vtt(dz, ["dz"], dz, ["dz"], off("xe"), ["xe"], mult)
+            spare = ([lambda b=b: units("e1", "c1", [b]) for b in (1, 2, 3)]
+                     + [lambda n=n: vts(pairs(n, None, 0, 2), [n + "0"], full("jj"), ["jj"], 0.0, None, mult) for n in ("dd", "tw")]
+                     + [lambda n=n, h=h, o=o: vtt(pairs(n, h, 1, 2), parts(n + "1", h), pl("lt", 0, h), ["lt"], pl("lt", 1, h), ["lt"], o)
+                        for n, o in (("tg", add), ("tw", sub)) for h in (0, 1)])
+        for h in (0, 1):
+            gather(h, full("t1"), parts("t1"), "o0", parts("o0", h), "t2")
+
+        def level(c, j):
+            h = half(c[1])
+            sn, o, t, nt, l, m, kj = "sc" if j % 2 else "sd", "o%d" % j, "t%d" % (j + 1), "t%d" % (j + 2), "l%d" % j, "l%d" % (j + 1), "k%d" % j
+            if c[0] == "s":
+                hold(sn, parts(sn, h), t, parts(t, h), h)
+            if c[0] == "t":
+                offsets(o, parts(o, h), sn, parts(sn, h), h)
+            if c[0] == "p":
+                acopy(full(nt, h), parts(nt, h), full(t).indirect(off(o, h)), parts(t) + parts(o, h))
+            if c[0] == "m":
+                vtt(full(m, h), parts(m, h), full(l).indirect(off(o, h)), parts(l) + parts(o, h), full(kj, h), parts(kj, h), amin)
+            if c[0] == "d":
+                vcopy(full(kj, h), parts(kj, h), full(l, h), parts(l, h))
+            if c[0] == "D":
+                acopy(full(kj, h), parts(kj, h), full(l, h), parts(l, h))
+            if c[0] == "K":
+                vtt(full("l2s", h), parts("l2s", h), pairs("pp", h, 1, 2), parts("pp", h), full("t1", h), parts("t1", h), amin)
+            if c[0] == "x" and spare:
+                spare.pop(0)()
+            if c[0] in "LM":
+                n = l if c[0] == "L" else kj
+                vtt(full(n, h), parts(n, h), full("l2s", h), parts("l2s", h), full("t2", h), parts("t2", h), amin)
+
+        for j in range(1, 7):
+            for c in (FIRST if j == 1 else LAST if j == 6 else ORDER).split():
+                level(c, j - (len(c) > 2))
+        while spare:
+            spare.pop(0)()
+        if k == 0:
+            own()
+        for b in range(4):
+            mm(4 + b, "c1", 128 * b, ["c1%d" % b], aq, asc, [aq])
+
+        o6k, zk, by, slot = parts("o6"), parts(zq), {1: ta, 2: tb, 3: td}, {}
+
+        def middle(c):
+            i, b = (int(c[1]), int(c[2])) if c[0] in "fsatT" and c[1].isdigit() else (0, 0)
+            x, z = "z%d" % (i - 1), "z%d" % i
+            out = el("z3", b) if i == 3 else pl(z, b)
+            if c == "l8":
+                vtt(full("l8"), ["l8"], full("l7").indirect(off("o6")), parts("l7") + o6k, full("l6"), parts("l6"), amin)
+            elif c == "hold":
+                hold("sa", ["sa"], "l8", ["l8"])
+            elif c == "o8":
+                offsets("o8", ["o8"], "sa", ["sa"])
+            elif c == "ne":
+                vtt(T.tz[:, 2:3 * K:3], ["tz2"], ends("sa"), ["sa"], off("cv"), ["cv"], ne)
+            elif c == "mini":
+                vscan(T.to[:, 0:3 * K], ["to"], T.tz[:, 0:3 * K], T.tp[:, 0:3 * K], ["tz0", "tz1", "tz2", "tp0", "tp1", "tp2"])
+            elif c == "pt":
+                vcopy(off(pt), [pt], T.to[:, 2:3 * K:3], ["to"])
+                send(dst, "ra%d" % k, [pt], off(ta), off(pt))
+            elif c[0] == "e":
+                h = half(c[1])
+                vtt(pairs("pp", h, 0, 2), parts("fl", h) + ["pe"], full("l8", h), ["l8"], full("ic", h), ["ic"], eq)
+            elif c[0] == "w":
+                h = half(c[1])
+                vscan(pairs("tq", h), parts("tq", h), pairs("dd", h), pairs("pp", h), ["dd0"] + parts("dd", h) + parts("fl", h) + parts("pp", h))
+            elif c == "p2":
+                vts(off("o9"), ["o9"], T.to[:, 2:3 * K:3], ["to"], 2.0, 1.0, mult, add)
+            elif c[0] == "q":
+                h = half(c[2])
+                win, wk, o, ok = (T.tq[:], parts("tq"), "o9", ["o9"]) if c[1] == "1" else (full("q1"), parts("q1"), pu, parts(pu, h))
+                gather(h, win, wk, o, ok, c[:2])
+            elif c[:2] in ("hu", "hv"):
+                h = half(c[2])
+                sn, q = ("sb", "q1") if c[1] == "u" else ("se", "q2")
+                hold(sn, parts(sn, h), q, parts(q, h), h)
+            elif c[:2] in ("tu", "tv"):
+                h = half(c[2])
+                sn, o = ("sb", pu) if c[1] == "u" else ("se", pv)
+                offsets(o, parts(o, h), sn, parts(sn, h), h)
+            elif c in ("Gu", "Gv"):
+                o, sem, far = (pu, "rb", tb) if c[1] == "u" else (pv, "rd", td)
+                send(dst, sem + str(k), parts(o), off(far), off(o))
+            elif c == "S1":
+                acopy(full("sl1"), ["sl1"], full("ssb").indirect(off("o8")), parts("ssb") + ["o8"])
+            elif c[0] == "S":
+                n, m = "sl" + c[1], "sl%d" % (int(c[1]) - 1)
+                acopy(full(n), [n], full(m).indirect(off("o6")), [m] + o6k)
+            elif c[0] == "c":
+                acopy(pl("z0", int(c[1])), ["z0" + c[1]], bank(4 + int(c[1])), ["ps%d" % (4 + int(c[1]))], 0.125)
+            elif c[0] == "F":
+                acopy(pl("fo", int(c[1])), ["fo" + c[1]], bank(int(c[1])), ["ps" + c[1]])
+            elif c[0] in "tT":
+                (vcopy if c[0] == "t" else acopy)(pl("zd", 4 * i + b), ["d" + c[1:]], pl(z, b), [z + c[2]])
+            elif c[0] == "s":
+                vtt(out, [z + c[2]], pl(x, b).indirect(off(by[i])), [x + c[2], by[i]], pl("zd", 4 * (i - 1) + b), ["d%d%d" % (i - 1, b)], add)
+            elif c[0] == "f":
+                slot[i, b] = len(slot)
+                acopy(pl("gb", slot[i, b]), ["gb%d" % slot[i, b]], pl(x, b).indirect(off(by[i])), [x + c[2], by[i]])
+            elif c[0] == "a":
+                h = half(c[3]) if len(c) > 3 else None
+                out = el("z3", b, h) if i == 3 else out
+                vtt(out, [z + c[2] + ("b" if h else "")], pl("gb", slot[i, b], h), ["gb%d" % slot[i, b]], pl(x, b, h), [x + c[2]], add)
+
+        for c in MIDDLE.split():
+            middle(c)
+            if last and c == "q1b":
+                vts(off("hd"), ["hd"], dz, ["dz"], 0.5, None, mult)
+
+        def state(c, last=last):
+            b, h = int(c[1]) if c[1].isdigit() else 0, half(c[-1]) if c[-1] in "ab" else None
+            if c[0] == "q":
+                quant_half("z3", ["z30", "z31", "z32", "z33"] + ["z32b", "z33b"] * h, zq, zs, h)
+                mm(4 * h, "wq", 0, ["wqc", "wqp"], zq, zs, [zk[h]], *halves[h])
+            elif c[0] == "m":
+                mm(4 + b, "wq", 128 * b, ["wqc", "wqp"], zq, zs, zk)
+            elif c == "cm":
+                vtt(full("cm"), ["cm"], full("sl3").indirect(off("o6")), ["sl3"] + o6k, full("ssb"), parts("ssb"), gt)
+            elif c == "hc":
+                hold("sf", ["sf"], "cm", ["cm"])
+            elif c == "xe":
+                op("A", ["sf", "thr"], ["xe"], lambda: A.activation(off("xe"), ends("sf"), sign, bias=T.thr[:, 0:1], scale=-1.0))
+            elif c == "dz":
+                n, key = (off("hd"), "hd") if last else (dz, "dz")
+                vtt(n, [key], n, [key], off("xe"), ["xe"], mult)
+            elif c == "xt" and not last:
+                op("A", ["cm"], ["xw"], lambda: A.activation(full("xw"), full("cm"), same, bias=1.0, scale=-2.0))
+            elif c == "hd" and not last:
+                vtt(pairs("tw", None, 1, 2), parts("tw1"), pairs("tw", None, 1, 2), parts("tw1"), full("xw"), ["xw"], mult)
+            elif c == "h0a":
+                acopy(T.hb[:, 0:CUT], ["hb0a"], bank(0, CUT), ["ps0"], 0.03125)
+            elif c == "h0b":
+                acopy(T.hb[:, CUT:C], ["hb0b"], bank(4, C - CUT), ["ps4"], 0.03125)
+            elif c[0] == "h" and c[1].isdigit():
+                acopy(pl("hb", b), ["hb%d" % b], bank(4 + b), ["ps%d" % (4 + b)], 0.03125)
+            elif c == "xg":
+                acopy(full("xg"), ["xg"], pl("hb", 3).indirect(off(pt)), ["hb3", pt])
+            elif c[:2] == "n3":
+                vtt(el(nx, 3, h), [nx + "_%d" % (3 + h)], full("xg", h), ["xg"], T.ps3[:, halves[h][0]:halves[h][1]], ["ps3"], add)
+            elif c[0] == "n":
+                vtt(el(nx, b), [nx + "_%d" % b], pl("hb", b).indirect(off(pt)), (["hb%d" % b] if b else parts("hb0")) + [pt], pl("fo", b), ["fo%d" % b], add)
+
+        later[:] = [state]
+        for c in STATE.split():
+            if c in LATER.split() and not last:
+                continue
+            state(c)
+            if last and c == "n1":
+                for h in (0, 1):
+                    vtt(T.lf[:, h * K:h * K + K], ["lf%d" % h], mid, ["mid"], off("hd"), ["hd"], add if h else sub)
+            if last and c == "n2":
+                vcopy(T.lo[:, 0:2 * K], ["lo"], T.lf[:, 0:2 * K], ["lf0", "lf1"])
+                acopy(T.lrep[:], ["lrep"], full("fi").indirect(T.lo[:, 0:2 * K]), ["fi", "lo"])
 
     xq, xs = "xq%d" % ROUNDS, "xs%d" % ROUNDS
     xk = parts(xq)
-    vts(off("hd"), ["hd"], dz, ["dz"], 0.5, None, mult)
     for h in (0, 1):
         quant_half("xt%d" % ROUNDS, ["xt%d_%d" % (ROUNDS, b) for b in range(4 + h)], xq, xs, h)
         mm(h, "vq", 0, ["vq"], xq, xs, [xk[h]], *halves[h])
-        vtt(off("l%df" % h), ["l%df" % h], mid, ["mid"], off("hd"), ["hd"], add if h else sub)
-    for h in (0, 1):
-        vcopy(T.lo[:, h * K:h * K + K], ["lo%d" % h], off("l%df" % h), ["l%df" % h])
     dma("Y", "doc", xk, [], T.oc[:], full(xq).bitcast(dt.uint8))
     for i in range(4):
         dma("Y", "dsc%d" % i, xk, [], T.osc[4 * i:4 * i + 4, :], T[xs][32 * i:32 * i + 4, :])
-    acopy(T.yo[:, 0:CUT], ["yo0"], bank(0, CUT), ["ps0"])
-    vcopy(T.yo[:, CUT:C], ["yo1"], bank(1, C - CUT), ["ps1"])
-    dma("A", "dy0", ["yo0"], [], T.y[:, 0:CUT], T.yo[:, 0:CUT])
-    dma("Y", "dy1", ["yo1"], [], T.y[:, CUT:C], T.yo[:, CUT:C])
-    acopy(T.lrep[:, 0:C], ["lrep0"], full("fi").indirect(T.lo[:, 0:K]), ["fi", "lo0"])
-    vcopy(T.lrep[:, C:2 * C], ["lrep1"], full("fi").indirect(T.lo[:, K:2 * K]), ["fi", "lo1"])
-    dma("A", "dls", ["lrep0", "lrep1"], [], T.ls[:], T.lrep[0:128:16, :])
+    dma("Y", "dls", ["lrep"], [], T.ls[:], T.lrep[0:128:16, :])
+    vcopy(T.yo[:, 0:CUT], ["yo0"], bank(0, CUT), ["ps0"])
+    acopy(T.yo[:, CUT:C], ["yo1"], bank(1, C - CUT), ["ps1"])
+    dma("A", "dy0", ["yo0", "yo1"], [], T.y[:], T.yo[:])
     for s in total:
         if known["Y"].get(s, 0) < total[s]:
             Q["Y"].wait_ge(T.sem[s], total[s])

from concourse.mybir import dt, AluOpType, ActivationFunctionType

C = 288
K = C // 16
STEP = [4, 1, 2]
ROUNDS = len(STEP)
HALF = C // 2
CUT = 160
LIFT = 512.0

SCORES = "ba bb ga gb ea eb wa wb dw sa sb pw keep"
FIRST = "Kw sb sa La tb pb ta pa Lb da db ma mb"
ORDER = "Da Db sa xw sb ta pa tb pb ma mb xw"
LAST = "Da Db sa xw sb ta tb ma mb"
MIDDLE = "l8 c0 c1 c2 c3 F0 F1 hold ea ne o8 eb S1 mini wa wb p2 pt q1a q1b t00 S2 huw tuw Gu q2b t01 q2a hvw tvw Gv f12 f13 s11 f21 a12 s10 a13 t10 a21 f22 s20 f23 a22 a23 f31 f32 t20 a31 s30 f33 S3 a32 a33a a33b F2"
STATE = "qa qb cm m1 m3 m2 h0a h0b hc h1 xe h3 h2 xg xt n0 dz n1 hd n2 n3a n3b"
LATER = "dz hd"

SCRATCH = {}


def _declare():
    s = SCRATCH
    for k in range(ROUNDS + 1):
        s["xt%d" % k] = ("sbuf", [128, 4 * C], "bfloat16")
        s["xq%d" % k] = ("sbuf", [128, C], "float8_e4m3fn_x4")
        s["xs%d" % k] = ("sbuf", [128, C], "uint8")
    for k in range(ROUNDS):
        s["aq%d" % k] = ("sbuf", [128, C], "float8_e4m3fn_x4")
        s["as%d" % k] = ("sbuf", [128, C], "uint8")
        for n in ("ta", "tb", "td"):
            s[n + str(k)] = ("sbuf", [128, 32], "uint16")
        s["zq%d" % k] = ("sbuf", [128, C], "float8_e4m3fn_x4")
        s["zs%d" % k] = ("sbuf", [128, C], "uint8")
    for n, w in (("ut", 512), ("vt", 512), ("en", 520), ("e1", 520), ("ic", C), ("mk", C), ("jj", C), ("m1", C), ("wa", C),
                 ("dw", C), ("cm", C), ("l2s", C), ("xw", C), ("pp", 2 * C), ("tq", 2 * C), ("lt", 2 * C),
                 ("q0", C), ("q1", C), ("q2", C), ("xg", C), ("tab", 24 * C), ("zd", 12 * C),
                 ("fo", 4 * C), ("z0", 4 * C), ("z1", 4 * C), ("z2", 4 * C), ("z3", 4 * C), ("gb", 12 * C), ("hb", 4 * C)):
        s[n] = ("sbuf", [128, w], "bfloat16")
    for n, w in (("sg", 2 * C), ("sw", 2 * C), ("sp", 2 * C), ("tg", 2 * C), ("tw", 2 * C), ("dd", 2 * C), ("tz", 64), ("tp", 64), ("to", 64),
                 ("sa", C), ("sb", C), ("sc", C), ("sd", C), ("se", C), ("sf", C), ("lm", C)):
        s[n] = ("sbuf", [128, w], "float16")
    for n, w in (("ol", 32 * 10), ("snt", 32 * 3 * ROUNDS), ("uo", 32), ("lo", 64), ("li", 64)):
        s[n] = ("sbuf", [128, w], "uint16")
    for n, w in (("pi", 8), ("pj", 8), ("k16", 24), ("uj", 8), ("la32", 24), ("lb32", 24)):
        s[n] = ("sbuf", [128, w], "int32")
    for n, w in (("ssb", C), ("sl1", C), ("sl2", C), ("sl3", C), ("fi", C), ("lrep", 2 * C), ("yo", C), ("sc0", 8), ("sc1", 8), ("thr", 8),
                 ("pf", 8), ("pn", 8), ("cw", 24), ("cv", 24), ("xe", 24), ("sm", 24), ("hd", 24), ("lf", 48)):
        s[n] = ("sbuf", [128, w], "float32")
    for n, w in (("uq", 128), ("uq2", 128), ("vq", 128), ("wq", 512), ("c1", 512)):
        s[n] = ("sbuf", [128, w], "float8_e4m3fn_x4")
        s[n + "s"] = ("sbuf", [128, w], "uint8")
    for i in range(8):
        s["ps%d" % i] = ("psum", [128, 512], "float32")


_declare()
SEMAPHORES = (["eV", "eA", "eP", "eG", "left", "left0", "left1"] + ["dx", "du", "dla", "dlb", "dwc", "dws", "dv", "dls", "doc", "dy0", "dy1"] + ["dsc%d" % i for i in range(4)]
              + ["%s%d" % (n, k) for n in ("rx", "ra", "rb", "rd") for k in range(ROUNDS)])


def rank_program(g, core, T, topo):
    rank = T.rank_of(core)
    if rank is None:
        return
    Q = {"V": g.vector, "A": g.scalar, "P": g.tensor, "G": g, "Y": g.sync}
    count, known, snap, lastw, readers, total = {}, {q: {} for q in Q}, {}, {}, {}, {}

    def wait_for(q, toks):
        best = {}
        for s, n in toks:
            best[s] = max(n, best.get(s, 0))
        todo = [(s, n) for s, n in best.items() if known[q].get(s, 0) < n]
        todo = [t for t in todo if not any(u != t and snap.get(u, {}).get(t[0], 0) >= t[1] for u in todo)]
        for s, n in todo:
            Q[q].wait_ge(T.sem[s], n)
            for a, b in list(snap.get((s, n), {}).items()) + [(s, n)]:
                known[q][a] = max(b, known[q].get(a, 0))

    def before(q, reads, writes):
        toks = []
        for b in reads:
            if b in lastw:
                toks.append(lastw[b])
            if b[:2] == "ps":
                toks += [t for t in readers.get(b, []) if t[0] != "e" + q]
        for b in writes:
            if b in lastw:
                toks.append(lastw[b])
            toks += readers.get(b, [])
        wait_for(q, toks)

    def after(q, tok, reads, writes):
        snap[tok] = dict(known[q])
        for b in reads:
            readers.setdefault(b, []).append(tok)
        for b in writes:
            lastw[b] = tok
            readers[b] = []

    def op(q, reads, writes, call):
        before(q, reads, writes)
        s = "e" + q
        count[s] = count.get(s, 0) + 1
        call().then_inc(T.sem[s], 1)
        total[s] = count[s]
        after(q, (s, count[s]), reads, writes)

    def dma(q, sem, reads, writes, out, in_):
        before(q, reads, writes)
        Q[q].dma_start(out, in_).then_inc(T.sem[sem], 16)
        total[sem] = 16
        after(q, (sem, 16), reads, writes)

    def send(dst, sem, reads, out, in_):
        before("G", reads, [])
        rid, pid = topo.addr(dst, core)
        left = {"rx0": "left0", "rx1": "left1"}.get(sem, "left")
        g.remote_dma(out, in_, T.sem[sem], T.sem[left], pid, rid, topo.mask(core, dst))
        total[left] = total.get(left, 0) + len(topo.engines(core, dst))

    def lands(src, sem, buf, writes=1):
        n = writes * len(topo.engines(src, core))
        total[sem] = n
        for b in buf:
            lastw[b] = (sem, n)
            readers[b] = []

    V, A, P = g.vector, g.scalar, g.tensor
    mult, add, sub, lt, gt, eq, ne, amin = (AluOpType.mult, AluOpType.add, AluOpType.subtract, AluOpType.is_lt, AluOpType.is_gt, AluOpType.is_equal,
                                            AluOpType.not_equal, AluOpType.min)
    copy, sign, same = ActivationFunctionType.Copy, ActivationFunctionType.Sign, ActivationFunctionType.Identity
    tables = {n: i * C for i, n in enumerate(["t%d" % i for i in range(9)] + ["l%d" % i for i in range(9)] + ["k%d" % i for i in range(1, 7)])}

    halves = ((0, CUT), (CUT, C))
    wide = (CUT, C - CUT)
    runs = ((0, CUT // 16), (CUT // 16, K))

    def parts(n, h=None):
        return [n + "a", n + "b"] if h is None else [n + "ab"[h]]

    def half(c):
        return None if c == "w" else "ab".index(c)

    def full(n, h=None):
        a, e = (0, C) if h is None else halves[h]
        if n in tables:
            return T.tab[:, tables[n] + a:tables[n] + e]
        return T[n][:, a:e]

    def pairs(n, h=None, first=0, step=1):
        a, e = (0, C) if h is None else halves[h]
        return T[n][:, 2 * a + first:2 * e:step]

    picks = {n: i * 32 for i, n in enumerate(["o%d" % i for i in range(10)])}
    sent = {n + str(i): (3 * i + j) * 32 for i in range(ROUNDS) for j, n in enumerate(["pt", "pu", "pv"])}

    def off(n, h=None):
        a, e = (0, K) if h is None else runs[h]
        if n in picks:
            return T.ol[:, picks[n] + a:picks[n] + e]
        if n in sent:
            return T.snt[:, sent[n] + a:sent[n] + e]
        return T[n][:, a:e]

    def pl(n, b, h=None):
        a, e = (0, C) if h is None else halves[h]
        return T[n][:, b * C + a:b * C + e]

    def el(n, b, h=None):
        a, e = (0, C) if h is None else halves[h]
        return T[n][:, 4 * a + b:4 * e:4]

    def ends(n, h=None):
        a, e = (0, C) if h is None else halves[h]
        return T[n][:, a + 15:e:16]

    def bank(i, w=C):
        return T["ps%d" % i][:, 0:w]

    def vtt(out, ok, a, ak, b, bk, o):
        op("V", ak + bk, ok, lambda: V.tensor_tensor(out, a, b, o))

    def vts(out, ok, a, ak, s1, s2, *o):
        op("V", ak, ok, lambda: V.tensor_scalar(out, a, s1, s2, *o))

    def vcopy(out, ok, in_, ik):
        op("V", ik, ok, lambda: V.tensor_copy(out, in_))

    def vscan(out, ok, d0, d1, ik):
        op("V", ik, ok, lambda: V.tensor_tensor_scan(out, d0, d1, 0.0, mult, add))

    def acopy(out, ok, in_, ik, scale=1.0):
        op("A", ik, ok, lambda: A.activation(out, in_, copy, scale=scale))

    def hold(sn, ok, src, sk, h=None):
        op("V", ["dw"] + sk, ok, lambda: V.tensor_tensor_scan(full(sn, h), full("dw", h), full(src, h), 0.0, add, AluOpType.max))

    def offsets(out, ok, sn, sk, h=None):
        vts(off(out, h), ok, ends(sn, h), sk + ["sc1"], T.sc1[:, 0:1], None, add)

    def gather(h, win, wk, o, ok, out):
        (vcopy if h else acopy)(full(out, h), parts(out, h), win.indirect(off(o, h)), wk + ok)

    def quant(t, tk, q, s, w=C):
        op("V", tk, [q], lambda: V.quantize_mx(T[q][:, 0:w], T[s][:, 0:w], T[t][:, 0:4 * w]))

    def quant_half(t, tk, q, s, h):
        a, e = halves[h]
        op("V", tk, parts(q, h), lambda: V.quantize_mx(T[q][:, a:e], T[s][:, a:e], T[t][:, 4 * a:4 * e]))

    def units(e, c, which=range(4)):
        for b in which:
            op("V", [e], [c + str(b)], lambda: V.quantize_mx(T[c][:, 128 * b:128 * b + 128], T[c + "s"][:, 128 * b:128 * b + 128],
                                                             T[e][:, 4 - b:4 - b + 512]))

    def mm(i, l, a, lk, r, rs, rk, c0=0, c1=C):
        op("P", lk + rk, ["ps%d" % i], lambda: P.matmul_mx(bank(i, c1 - c0), T[l][:, a:a + 128], T[l + "s"][:, a:a + 128],
                                                           T[r][:, c0:c1], T[rs][:, c0:c1], True, True))

    def iota(out, ok, pattern, base, cm):
        op("G", [], [ok], lambda: g.iota(out, pattern, base, cm, allow_small_or_imprecise_dtypes=True))

    dma("Y", "dx", [], ["xt0"], T.xt0[:], T.x[:])
    dma("A", "du", [], ["ut"], T.ut[:], T.u[:])
    dma("Y", "dla", [], ["la32"], off("la32"), T.la[:])
    dma("A", "dlb", [], ["lb32"], off("lb32"), T.lb[:])
    op("V", [], ["en"], lambda: V.memset(T.en[:], 1.0))
    iota(T.pi[:, 0:1], "pi", [[0, 1]], 0, 1)
    iota(T.uj[:, 0:8], "uj", [[16, 8]], 0, 0)
    iota(off("k16"), "k16", [[16, K]], 0, 0)
    iota(T.jj[:], "jj", [[0, K], [1, 16]], 0, 0)
    op("G", ["en"], ["e1"], lambda: g.affine_select(T.e1[:], T.en[:], [[1, 520]], eq, 0.0, -4, -4))
    iota(T.ic[:], "ic", [[1, C]], -HALF, 0)

    s1, pf, pn = T.sc1[:, 0:1], T.pf[:, 0:1], T.pn[:, 0:1]
    dz, mid = T.sw[:, 31:2 * C:32], T.sg[:, 31:2 * C:32]
    vts(T.pj[:, 0:1], ["pj"], T.pi[:, 0:1], ["pi"], 15, None, AluOpType.bitwise_and)
    vcopy(T.uo[:, 0:8], ["uo"], T.uj[:, 0:8], ["uj"])
    vts(T.tz[:, 0:3 * K:3], ["tz0"], off("k16"), ["k16"], 0.0, None, mult)
    vcopy(pf, ["pf"], T.pj[:, 0:1], ["pj"])
    vts(pn, ["pn"], T.pj[:, 0:1], ["pj"], 1.0, None, add)
    vts(T.sc0[:, 0:1], ["sc0"], T.pj[:, 0:1], ["pj"], 15.0, LIFT, ne, mult)
    vts(T.tz[:, 1:3 * K:3], ["tz1"], off("k16"), ["k16"], 0.0, 1.0, mult, add)
    vts(off("cw"), ["cw"], off("k16"), ["k16", "pf"], pf, None, add)
    vts(s1, ["sc1"], T.sc0[:, 0:1], ["sc0"], -1.0, float(HALF), mult, add)
    vts(T.thr[:, 0:1], ["thr"], T.sc0[:, 0:1], ["sc0"], 0.5, None, add)
    vts(T.tp[:, 1:3 * K:3], ["tp1"], off("cw"), ["cw"], -1.0, None, mult)
    vcopy(T.tp[:, 2:3 * K:3], ["tp2"], off("cw"), ["cw"])
    vts(off("cv"), ["cv"], off("cw"), ["cw", "sc1"], s1, None, sub)
    vts(pairs("sw", None, 1, 2), ["dz"], full("jj"), ["jj"], 0.0, 1.0, mult, add)
    vts(pairs("sg", None, 1, 2), ["mid"], full("jj"), ["jj"], 0.0, -0.5, eq, mult)
    vts(pairs("sw", None, 0, 2), ["sw"], full("jj"), ["jj"], 0.0, None, ne)
    vts(full("mk"), ["mk"], full("jj"), ["jj", "pf"], pf, -1e29, ne, mult)
    vts(full("m1"), ["m1"], full("jj"), ["jj", "pf"], pf, -16384.0, eq, mult)
    vts(full("wa"), ["wa"], full("jj"), ["jj", "pn"], pn, LIFT, eq, mult)
    quant("ut", ["ut"], "uq", "uqs", 128)
    vtt(full("dw"), ["dw"], full("wa"), ["wa"], full("m1"), ["m1"], add)
    vcopy(T.uq2[:, 0:128].bitcast(dt.uint32), ["uq2c"], T.uq[:, 0:128].bitcast(dt.uint32).indirect(T.uo[:, 0:8]), ["uq", "uo"])
    op("A", ["uq", "uo"], ["uq2p"], lambda: A.activation(T.uq2s[:, 0:128], T.uqs[:, 0:128].indirect(T.uo[:, 0:8]), copy))

    later = []
    for k in range(ROUNDS):
        dst, src = T.cores[(rank + STEP[k]) % 8], T.cores[(rank - STEP[k]) % 8]
        xt, xq, xs, aq, asc, zq, zs = [n + str(k) for n in ("xt", "xq", "xs", "aq", "as", "zq", "zs")]
        ta, tb, td, pt, pu, pv = [n + str(k) for n in ("ta", "tb", "td", "pt", "pu", "pv")]
        nx = "xt%d" % (k + 1)
        last = k == ROUNDS - 1
        lands(src, "rx%d" % k, [aq], 2)
        lands(src, "ra%d" % k, [ta])
        lands(src, "rb%d" % k, [tb])
        lands(src, "rd%d" % k, [td])

        xk = parts(xq)

        def own():
            for b in range(4):
                mm(b, "c1", 128 * b, ["c1%d" % b], xq, xs, xk)

        for h in (0, 1):
            quant_half(xt, [xt] + [xt + "_%d" % b for b in range(4 + h)], xq, xs, h)
            for i in (4 + h, 6 + h):
                mm(i, "uq2", 0, ["uq2c", "uq2p"], xq, xs, [xk[h]], *halves[h])
        for c in LATER.split() if k else []:
            later[0](c)
        send(dst, "rx%d" % k, xk, full(aq).bitcast(dt.uint8), full(xq).bitcast(dt.uint8))
        send(dst, "rx%d" % k, xk, full(asc), full(xs))
        if k:
            own()
        else:
            iota(T.fi[:], "fi", [[1, C]], 0, 0)
            vtt(off("sm"), ["sm"], off("la32"), ["la32"], off("lb32"), ["lb32"], add)
            vtt(dz, ["dz"], off("lb32"), ["lb32"], off("la32"), ["la32"], sub)
            vcopy(T.li[:, 0:K], ["lia"], off("la32"), ["la32"])
            vcopy(T.li[:, K:2 * K], ["lib"], off("lb32"), ["lb32"])
            vts(mid, ["mid"], off("sm"), ["sm"], 0.5, None, mult)
        if k < 2:
            wait_for("Y", [("left%d" % k, total["left%d" % k])])
            if k:
                dma("Y", "dv", [], ["vt"], T.vt[:], T.v[:])
            else:
                dma("Y", "dwc", [], ["wqc"], T.wq[:].bitcast(dt.uint8), T.wc[:])
                dma("Y", "dws", [], ["wqp"], T.wqs[:], T.ws[:])

        def scores(c):
            h = half(c[1]) if len(c) == 2 else None
            if c[0] == "b":
                vtt(pairs("sg", h, 0, 2), parts("sg", h), bank(4 + h, wide[h]), ["ps%d" % (4 + h)], full("mk", h), ["mk"], lt)
            if c[0] == "e":
                vscan(pairs("sp", h), parts("sp", h), pairs("sw", h), pairs("sg", h), ["sw", "dz", "mid"] + parts("sg", h))
            if c[0] == "p":
                vcopy(off("o0", h), parts("o0", h), pairs("sp", h, 31, 32), parts("sp", h))
            if c[0] == "s":
                acopy(full("ssb", h), parts("ssb", h), bank(6 + h, wide[h]), ["ps%d" % (6 + h)])
            if c == "keep":
                vcopy(T.tp[:, 0:3 * K:3], ["tp0"], pairs("sp", None, 31, 32), parts("sp"))
            if k and c[0] == "g":
                op("A", ["ps%d" % (6 + h)], parts("tg", h), lambda: A.activation(pairs("tg", h, 0, 2), bank(6 + h, wide[h]), sign, bias=2.0 ** -93))
            if k and c[0] == "w":
                vscan(pairs("pp", h), parts("pp", h) + parts("fl", h), pairs("tw", h), pairs("tg", h), ["tw0"] + parts("tw1", h) + parts("tg1", h) + parts("tg", h))
            if c[0] == "d":
                vts(off("o7", h), parts("o7", h), pairs("sp", h, 31, 32), parts("sp", h), 2.0, 1.0, mult, add)

        for c in SCORES.split():
            if k == 0 and c == "sb":
                acopy(T.lt[:], ["lt"], full("ic").indirect(T.li[:, 0:2 * K]), ["ic", "lia", "lib"], 0.5)
            else:
                scores(c)

        if k == 0:
            for h in (0, 1):
                (vcopy if h else acopy)(pairs("pp", h, 1, 2), parts("pp", h), full("ic").indirect(off("o0", h)), ["ic"] + parts("o0", h))
            scores("sb")
            vts(pairs("pp", None, 0, 2), ["pe"], full("jj"), ["jj"], 0.0, None, mult)
            units("e1", "c1", [0])
        for h in (0, 1):
            gather(h, T.pp[:], parts("pp") + ["pe"], "o7", parts("o7", h), "t1")
        vtt(pairs("dd", None, 1, 2), parts("dd"), full("ic"), ["ic"], pairs("pp", None, 1, 2), parts("pp"), sub)
        spare = [lambda: quant("vt", ["vt"], "vq", "vqs", 128)] if last else []
        if k == 0:
            spare = ([lambda b=b: units("e1", "c1", [b]) for b in (1, 2, 3)]
                     + [lambda n=n: vts(pairs(n, None, 0, 2), [n + "0"], full("jj"), ["jj"], 0.0, None, mult) for n in ("dd", "tw")]
                     + [lambda n=n, h=h, o=o: vtt(pairs(n, h, 1, 2), parts(n + "1", h), pl("lt", 0, h), ["lt"], pl("lt", 1, h), ["lt"], o)
                        for n, o in (("tg", add), ("tw", sub)) for h in (0, 1)])
        for h in (0, 1):
            gather(h, full("t1"), parts("t1"), "o0", parts("o0", h), "t2")

        def level(c, j):
            h = half(c[1])
            sn, o, t, nt, l, m, kj = "sc" if j % 2 else "sd", "o%d" % j, "t%d" % (j + 1), "t%d" % (j + 2), "l%d" % j, "l%d" % (j + 1), "k%d" % j
            if c[0] == "s":
                hold(sn, parts(sn, h), t, parts(t, h), h)
            if c[0] == "t":
                offsets(o, parts(o, h), sn, parts(sn, h), h)
            if c[0] == "p":
                acopy(full(nt, h), parts(nt, h), full(t).indirect(off(o, h)), parts(t) + parts(o, h))
            if c[0] == "m":
                vtt(full(m, h), parts(m, h), full(l).indirect(off(o, h)), parts(l) + parts(o, h), full(kj, h), parts(kj, h), amin)
            if c[0] == "d":
                vcopy(full(kj, h), parts(kj, h), full(l, h), parts(l, h))
            if c[0] == "D":
                acopy(full(kj, h), parts(kj, h), full(l, h), parts(l, h))
            if c[0] == "K":
                vtt(full("l2s", h), parts("l2s", h), pairs("pp", h, 1, 2), parts("pp", h), full("t1", h), parts("t1", h), amin)
            if c[0] == "x" and spare:
                spare.pop(0)()
            if c[0] in "LM":
                n = l if c[0] == "L" else kj
                vtt(full(n, h), parts(n, h), full("l2s", h), parts("l2s", h), full("t2", h), parts("t2", h), amin)

        for j in range(1, 7):
            for c in (FIRST if j == 1 else LAST if j == 6 else ORDER).split():
                level(c, j - (len(c) > 2))
        while spare:
            spare.pop(0)()
        if k == 0:
            own()
        for b in range(4):
            mm(4 + b, "c1", 128 * b, ["c1%d" % b], aq, asc, [aq])

        o6k, zk, by, slot = parts("o6"), parts(zq), {1: ta, 2: tb, 3: td}, {}

        def middle(c):
            i, b = (int(c[1]), int(c[2])) if c[0] in "fsatT" and c[1].isdigit() else (0, 0)
            x, z = "z%d" % (i - 1), "z%d" % i
            out = el("z3", b) if i == 3 else pl(z, b)
            if c == "l8":
                vtt(full("l8"), ["l8"], full("l7").indirect(off("o6")), parts("l7") + o6k, full("l6"), parts("l6"), amin)
            elif c == "hold":
                hold("sa", ["sa"], "l8", ["l8"])
            elif c == "o8":
                offsets("o8", ["o8"], "sa", ["sa"])
            elif c == "ne":
                vtt(T.tz[:, 2:3 * K:3], ["tz2"], ends("sa"), ["sa"], off("cv"), ["cv"], ne)
            elif c == "mini":
                vscan(T.to[:, 0:3 * K], ["to"], T.tz[:, 0:3 * K], T.tp[:, 0:3 * K], ["tz0", "tz1", "tz2", "tp0", "tp1", "tp2"])
            elif c == "pt":
                vcopy(off(pt), [pt], T.to[:, 2:3 * K:3], ["to"])
                send(dst, "ra%d" % k, [pt], off(ta), off(pt))
            elif c[0] == "e":
                h = half(c[1])
                vtt(pairs("pp", h, 0, 2), parts("fl", h) + ["pe"], full("l8", h), ["l8"], full("ic", h), ["ic"], eq)
            elif c[0] == "w":
                h = half(c[1])
                vscan(pairs("tq", h), parts("tq", h), pairs("dd", h), pairs("pp", h), ["dd0"] + parts("dd", h) + parts("fl", h) + parts("pp", h))
            elif c == "p2":
                vts(off("o9"), ["o9"], T.to[:, 2:3 * K:3], ["to"], 2.0, 1.0, mult, add)
            elif c[0] == "q":
                h = half(c[2])
                win, wk, o, ok = (T.tq[:], parts("tq"), "o9", ["o9"]) if c[1] == "1" else (full("q1"), parts("q1"), pu, parts(pu, h))
                gather(h, win, wk, o, ok, c[:2])
            elif c[:2] in ("hu", "hv"):
                h = half(c[2])
                sn, q = ("sb", "q1") if c[1] == "u" else ("se", "q2")
                hold(sn, parts(sn, h), q, parts(q, h), h)
            elif c[:2] in ("tu", "tv"):
                h = half(c[2])
                sn, o = ("sb", pu) if c[1] == "u" else ("se", pv)
                offsets(o, parts(o, h), sn, parts(sn, h), h)
            elif c in ("Gu", "Gv"):
                o, sem, far = (pu, "rb", tb) if c[1] == "u" else (pv, "rd", td)
                send(dst, sem + str(k), parts(o), off(far), off(o))
            elif c == "S1":
                acopy(full("sl1"), ["sl1"], full("ssb").indirect(off("o8")), parts("ssb") + ["o8"])
            elif c[0] == "S":
                n, m = "sl" + c[1], "sl%d" % (int(c[1]) - 1)
                acopy(full(n), [n], full(m).indirect(off("o6")), [m] + o6k)
            elif c[0] == "c":
                acopy(pl("z0", int(c[1])), ["z0" + c[1]], bank(4 + int(c[1])), ["ps%d" % (4 + int(c[1]))], 0.125)
            elif c[0] == "F":
                acopy(pl("fo", int(c[1])), ["fo" + c[1]], bank(int(c[1])), ["ps" + c[1]])
            elif c[0] in "tT":
                (vcopy if c[0] == "t" else acopy)(pl("zd", 4 * i + b), ["d" + c[1:]], pl(z, b), [z + c[2]])
            elif c[0] == "s":
                vtt(out, [z + c[2]], pl(x, b).indirect(off(by[i])), [x + c[2], by[i]], pl("zd", 4 * (i - 1) + b), ["d%d%d" % (i - 1, b)], add)
            elif c[0] == "f":
                slot[i, b] = len(slot)
                acopy(pl("gb", slot[i, b]), ["gb%d" % slot[i, b]], pl(x, b).indirect(off(by[i])), [x + c[2], by[i]])
            elif c[0] == "a":
                h = half(c[3]) if len(c) > 3 else None
                out = el("z3", b, h) if i == 3 else out
                vtt(out, [z + c[2] + ("b" if h else "")], pl("gb", slot[i, b], h), ["gb%d" % slot[i, b]], pl(x, b, h), [x + c[2]], add)

        for c in MIDDLE.split():
            middle(c)
            if last and c == "q1b":
                vts(off("hd"), ["hd"], dz, ["dz"], 0.5, None, mult)

        def state(c, last=last):
            b, h = int(c[1]) if c[1].isdigit() else 0, half(c[-1]) if c[-1] in "ab" else None
            if c[0] == "q":
                quant_half("z3", ["z30", "z31", "z32", "z33"] + ["z32b", "z33b"] * h, zq, zs, h)
                mm(4 * h, "wq", 0, ["wqc", "wqp"], zq, zs, [zk[h]], *halves[h])
            elif c[0] == "m":
                mm(4 + b, "wq", 128 * b, ["wqc", "wqp"], zq, zs, zk)
            elif c == "cm":
                vtt(full("cm"), ["cm"], full("sl3").indirect(off("o6")), ["sl3"] + o6k, full("ssb"), parts("ssb"), gt)
            elif c == "hc":
                hold("sf", ["sf"], "cm", ["cm"])
            elif c == "xe":
                op("A", ["sf", "thr"], ["xe"], lambda: A.activation(off("xe"), ends("sf"), sign, bias=T.thr[:, 0:1], scale=-1.0))
            elif c == "dz":
                n, key = (off("hd"), "hd") if last else (dz, "dz")
                vtt(n, [key], n, [key], off("xe"), ["xe"], mult)
            elif c == "xt" and not last:
                op("A", ["cm"], ["xw"], lambda: A.activation(full("xw"), full("cm"), same, bias=1.0, scale=-2.0))
            elif c == "hd" and not last:
                vtt(pairs("tw", None, 1, 2), parts("tw1"), pairs("tw", None, 1, 2), parts("tw1"), full("xw"), ["xw"], mult)
            elif c == "h0a":
                acopy(T.hb[:, 0:CUT], ["hb0a"], bank(0, CUT), ["ps0"], 0.03125)
            elif c == "h0b":
                acopy(T.hb[:, CUT:C], ["hb0b"], bank(4, C - CUT), ["ps4"], 0.03125)
            elif c[0] == "h" and c[1].isdigit():
                acopy(pl("hb", b), ["hb%d" % b], bank(4 + b), ["ps%d" % (4 + b)], 0.03125)
            elif c == "xg":
                acopy(full("xg"), ["xg"], pl("hb", 3).indirect(off(pt)), ["hb3", pt])
            elif c[:2] == "n3":
                vtt(el(nx, 3, h), [nx + "_%d" % (3 + h)], full("xg", h), ["xg"], T.ps3[:, halves[h][0]:halves[h][1]], ["ps3"], add)
            elif c[0] == "n":
                vtt(el(nx, b), [nx + "_%d" % b], pl("hb", b).indirect(off(pt)), (["hb%d" % b] if b else parts("hb0")) + [pt], pl("fo", b), ["fo%d" % b], add)

        later[:] = [state]
        for c in STATE.split():
            if c in LATER.split() and not last:
                continue
            state(c)
            if last and c == "n1":
                for h in (0, 1):
                    vtt(T.lf[:, h * K:h * K + K], ["lf%d" % h], mid, ["mid"], off("hd"), ["hd"], add if h else sub)
            if last and c == "n2":
                vcopy(T.lo[:, 0:2 * K], ["lo"], T.lf[:, 0:2 * K], ["lf0", "lf1"])
                acopy(T.lrep[:], ["lrep"], full("fi").indirect(T.lo[:, 0:2 * K]), ["fi", "lo"])

    xq, xs = "xq%d" % ROUNDS, "xs%d" % ROUNDS
    xk = parts(xq)
    for h in (0, 1):
        quant_half("xt%d" % ROUNDS, ["xt%d_%d" % (ROUNDS, b) for b in range(4 + h)], xq, xs, h)
        mm(h, "vq", 0, ["vq"], xq, xs, [xk[h]], *halves[h])
    dma("Y", "doc", xk, [], T.oc[:], full(xq).bitcast(dt.uint8))
    for i in range(4):
        dma("Y", "dsc%d" % i, xk, [], T.osc[4 * i:4 * i + 4, :], T[xs][32 * i:32 * i + 4, :])
    dma("Y", "dls", ["lrep"], [], T.ls[:], T.lrep[0:128:16, :])
    vcopy(T.yo[:, 0:CUT], ["yo0"], bank(0, CUT), ["ps0"])
    acopy(T.yo[:, CUT:C], ["yo1"], bank(1, C - CUT), ["ps1"])
    dma("A", "dy0", ["yo0", "yo1"], [], T.y[:], T.yo[:])
    for s in total:
        if known["Y"].get(s, 0) < total[s]:
            Q["Y"].wait_ge(T.sem[s], total[s])
